import numpy as np
import ml_dtypes


def mxq(x, axis, fmt="e4m3"):
    dtype, down = {"e4m3": (ml_dtypes.float8_e4m3fn, 7), "e5m2": (ml_dtypes.float8_e5m2, 14)}[fmt]
    v = np.moveaxis(np.asarray(x, np.float32).astype(ml_dtypes.bfloat16).astype(np.float64), axis, -1)
    blocks = v.reshape(v.shape[:-1] + (-1, 32))
    amax = np.abs(blocks).max(-1, keepdims=True)
    byte = np.maximum(np.where(amax > 0, np.frexp(amax)[1] - 1 + 127, 0) - down, 1)
    scale = np.exp2(byte - 127.0)
    codes = (blocks / scale).astype(np.float32).astype(dtype).astype(np.float64)
    return np.moveaxis((codes * scale).reshape(v.shape), -1, axis)


WIDE = False


def mx_kscale(k):
    if not WIDE:
        return np.ones(k)
    levels = np.array([10, -10, 5, -5, 0])
    if k % 512:
        return np.exp2(np.random.permutation(np.resize(levels, k // 32))).repeat(32)
    a = np.empty((k // 512, 16))
    for p in range(k // 512):
        a[p, :8] = np.random.permutation(np.resize(levels, 8))
        for g in range(8):
            far = levels[np.abs(levels - a[p, g]) >= 10]
            a[p, g + 8] = far[np.random.randint(len(far))]
    return np.exp2(a.ravel()).repeat(32)


def f64(x):
    return np.asarray(x).astype(np.float64)


def striped(idx):
    return np.tile(idx.reshape(-1, 16).T, (8, 1)).astype(np.uint16)


def unstriped(offs):
    return offs[:16].T.reshape(-1).astype(np.int64)


E2M1 = np.array([0.0, 0.5, 1.0, 1.5, 2.0, 3.0, 4.0, 6.0, -0.0, -0.5, -1.0, -1.5, -2.0, -3.0, -4.0, -6.0])


def pack_weight(w, fmt):
    k, n = w.shape
    w = f64(np.asarray(w, np.float32).astype(ml_dtypes.bfloat16)).reshape(k // 32, 32, n)
    amax = np.abs(w).max(1)
    if fmt == "e4m3":
        byte = np.frexp(amax)[1] - 1 + 127 - 7
    else:
        mant, ex = np.frexp(amax / 6.0)
        byte = np.where(mant > 0.5, ex, ex - 1) + 127
    byte = np.clip(np.where(amax > 0, byte, 1), 1, 254)
    scaled = (w * np.exp2(127.0 - byte)[:, None, :]).reshape(k, n).astype(np.float32)
    by_word = np.ascontiguousarray(scaled.reshape(k // 512, 128, 4, n).transpose(0, 1, 3, 2))
    if fmt == "e4m3":
        words = by_word.astype(ml_dtypes.float8_e4m3fn).view(np.uint8)
    else:
        c = by_word.astype(ml_dtypes.float4_e2m1fn).view(np.uint8) & 0xF
        words = (c[..., 0::2] | (c[..., 1::2] << 4)).reshape(k // 512, 128, 2 * n)
    return np.ascontiguousarray(words), np.ascontiguousarray(byte.astype(np.uint8).reshape(k // 512, 16, n))


def unpack_weight(words, scales, fmt):
    g, _, n = scales.shape
    words = np.ascontiguousarray(words).reshape(g, 128, n, -1)
    if fmt == "e4m3":
        vals = words.view(ml_dtypes.float8_e4m3fn).astype(np.float64)
    else:
        nib = np.empty((g, 128, n, 4), np.uint8)
        nib[..., 0::2] = words & 0xF
        nib[..., 1::2] = words >> 4
        vals = E2M1[nib]
    vals = vals * np.repeat(np.exp2(scales.astype(np.float64) - 127.0), 8, axis=1)[..., None]
    return vals.transpose(0, 1, 3, 2).reshape(g * 512, n)


K, T, E, C, N = 1536, 640, 20, 128, 256
TOP = 4


def by_expert(wq, xq):
    return np.concatenate([wq[e].T @ xq[:, e * C:(e + 1) * C] for e in range(E)], axis=1)


def setup_inputs():
    n = np.random.standard_normal
    s = mx_kscale(K)[:, None]
    deal = np.repeat(np.arange(E), C).reshape(TOP, T)[:, np.random.permutation(T)]
    deal = np.take_along_axis(deal, np.argsort(np.random.rand(TOP, T), axis=0), axis=0)
    for _ in range(8):
        s_, t_ = np.random.permutation(T).reshape(2, -1); r = np.random.randint(TOP, size=T // 2); x, y = deal[r, s_].copy(), deal[r, t_].copy()
        ok = ~((deal[:, s_] == y).any(0) | (deal[:, t_] == x).any(0)); deal[r[ok], s_[ok]] = y[ok]; deal[r[ok], t_[ok]] = x[ok]
    order = np.lexsort((np.random.rand(TOP * T), deal.reshape(-1)))
    slot_token = order % T; pos = np.empty(TOP * T, np.int64); pos[order] = np.arange(TOP * T); pos = pos.reshape(TOP, T)
    g = np.random.uniform(0.5, 1.5, (TOP, T)); g = g / g.sum(0)
    x = pack_weight(n((K, T)) * s, "e4m3")
    return {
        "x_words": x[0],
        "x_scales": x[1],
        "w": (n((E + 1, K, N)) / np.sqrt(K) / s[None]).astype(np.float32),
        "b": (0.3 * n((N, E + 1))).astype(np.float32),
        "gate": np.stack([np.tile(r, (N, 1)) for r in g]).astype(np.float32),
        "offs": striped(slot_token),
        "pos1": striped(pos[0]),
        "pos2": striped(pos[1]),
        "pos3": striped(pos[2]),
        "pos4": striped(pos[3]),
    }


def reference(x_words, x_scales, w, b, gate, offs, pos1, pos2, pos3, pos4):
    idx = unstriped(offs)
    wq = mxq(f64(w), 1, "e4m3")
    xs = unpack_weight(x_words, x_scales, "e4m3")
    ys = (wq[E].T @ xs) + f64(b)[:, E:]
    xq = unpack_weight(x_words, x_scales, "e4m3")[:, idx]
    y = by_expert(wq, xq)
    y = y + np.repeat(f64(b)[:, :E], C, axis=1)
    return ys + sum(f64(gate[r]) * y[:, unstriped(p)] for r, p in enumerate((pos1, pos2, pos3, pos4)))

@@ -1,0 +1,261 @@
+from contextlib import ExitStack
+
+import concourse.mybir as mybir
+from concourse.masks import make_identity
+
+K, T, E, C, N = 1536, 640, 20, 128, 256
+TOP = 4
+FLOPS = 2 * K * N * (E * C + T)
+
+F32 = mybir.dt.float32
+BF16 = mybir.dt.bfloat16
+I32 = mybir.dt.int32
+U32 = mybir.dt.uint32
+U16 = mybir.dt.uint16
+U8 = mybir.dt.uint8
+FP8X4 = mybir.dt.float8_e4m3fn_x4
+COPY = mybir.ActivationFunctionType.Copy
+IDENTITY = mybir.ActivationFunctionType.Identity
+MULT = mybir.AluOpType.mult
+ADD = mybir.AluOpType.add
+
+P = 128
+PACK = 4
+PASSES = K // (P * PACK)
+HALVES = N // P
+SLOTS = E * C
+SHARED = E
+GATHER = 512
+WINDOW = 704
+SPLIT = 0
+TOKEN_CHUNKS = ((0, 256), (256, 256), (512, 128))
+
+
+def tile_moe_shr_lin_bias_kernel(
+    tc, x_words, x_scales, w, b, gate, offs, pos1, pos2, pos3, pos4, out
+):
+    nc = tc.nc
+    with ExitStack() as ctx:
+        keep = ctx.enter_context(tc.tile_pool(name="keep", bufs=1))
+        ring = ctx.enter_context(tc.tile_pool(name="ring", bufs=2))
+        psum = ctx.enter_context(tc.psum_pool(name="psum", bufs=2))
+
+        offs_sb = keep.tile([P, SLOTS // 16], U16, name="offs_sb")
+        pos_sb = [keep.tile([P, T // 16], U16, name="pos_sb%d" % r) for r in range(TOP)]
+        words = keep.tile([P, (PASSES - 1) * T + WINDOW], I32, name="words", align_bytes=64)
+        planes = keep.tile([P, WINDOW], U8, name="planes", align_bytes=64)
+        bias = keep.tile([P, HALVES, 24], F32, name="bias")
+        gate_rows = keep.tile([P, P], F32, name="gate_rows")
+        gate_cols = keep.tile([P, 24], F32, name="gate_cols")
+        gate_sb = keep.tile([P, TOP * T], F32, name="gate_sb")
+        ident = keep.tile([P, P], F32, name="ident")
+        y = [keep.tile([P, SLOTS], F32, name="y%d" % h) for h in range(HALVES)]
+        ys = [keep.tile([P, T], F32, name="ys%d" % h) for h in range(HALVES)]
+
+        nc.vector.memset(planes[:].bitcast(I32), 0)
+        nc.vector.memset(words[:, PASSES * T :], 0)
+        nc.gpsimd.memset(gate_rows[:], 0.0)
+        make_identity(nc, ident[:])
+
+        def load_whole(e):
+            raw = ring.tile([P, PASSES, PACK * N], F32, name="raw", bufs=5)
+            nc.sync.dma_start(out=raw[:], in_=w[e].rearrange("(o p j) n -> p o (j n)", p=P, j=PACK))
+            return [raw[:, o, :].rearrange("p (j n) -> p j n", j=PACK) for o in range(PASSES)]
+
+        def load_pass(e, o, halves):
+            width = len(halves) * P
+            raw_pass = ring.tile([P, PACK, width], F32, name="raw_pass", bufs=6)
+            rows = w[e, o * P * PACK : (o + 1) * P * PACK, halves[0] * P : halves[0] * P + width]
+            nc.sync.dma_start(out=raw_pass[:], in_=rows.rearrange("(p j) n -> p j n", j=PACK))
+            return raw_pass[:]
+
+        def cast(engine, dst, src):
+            dst = dst.rearrange("p (c i j) -> p c j i", i=4, j=PACK)
+            src = src.rearrange("p j (c i) -> p c j i", i=4)
+            if engine == "S":
+                nc.scalar.activation(out=dst, in_=src, func=COPY)
+            else:
+                nc.vector.tensor_copy(out=dst, in_=src)
+
+        def quantize(raws, width, scalar_cols):
+            codes = ring.tile([P, PASSES * width], U32, name="codes", bufs=4, align_bytes=64)
+            scales = ring.tile([P, PASSES * width], U8, name="scales", bufs=4, align_bytes=64)
+            front = ring.tile([P, 2 * PACK * width], BF16, name="front", bufs=4, align_bytes=64)
+            last = ring.tile([P, PACK * width], BF16, name="last", bufs=4, align_bytes=64)
+            for o in range(2):
+                cast("S", front[:, o * PACK * width : (o + 1) * PACK * width], raws[o])
+            if scalar_cols > 0:
+                cast("S", last[:, : PACK * scalar_cols], raws[2][:, :, :scalar_cols])
+            if scalar_cols < width:
+                cast("V", last[:, PACK * scalar_cols :], raws[2][:, :, scalar_cols:])
+            nc.vector.quantize_mx(out=codes[:, : 2 * width].bitcast(FP8X4), scales=scales[:, : 2 * width], in_=front[:])
+            nc.vector.quantize_mx(out=codes[:, 2 * width :].bitcast(FP8X4), scales=scales[:, 2 * width :], in_=last[:])
+            return codes, scales
+
+        def gather_tokens(g):
+            slot_words = ring.tile([P, PASSES * GATHER], U32, name="slot_words", align_bytes=64)
+            slot_planes = ring.tile([P, GATHER], U8, name="slot_planes", align_bytes=64)
+            entries = offs_sb[:, g * GATHER // 16 : (g + 1) * GATHER // 16]
+            nc.vector.tensor_copy(out=slot_planes[:], in_=planes[:].indirect(entries))
+            for o in range(PASSES):
+                window = words[:, o * T : o * T + WINDOW].bitcast(U32)
+                nc.vector.tensor_copy(out=slot_words[:, o * GATHER : (o + 1) * GATHER], in_=window.indirect(entries))
+            return slot_words, slot_planes
+
+        def one_pass(acc, o, codes, scales, width, i, moving, moving_planes, stride, first, count):
+            cols = slice(o * width + i * P, o * width + (i + 1) * P)
+            nc.tensor.matmul_mx(
+                out=acc,
+                lhsT=codes[:, cols].bitcast(FP8X4),
+                lhsT_scale=scales[:, cols],
+                rhs=moving[:, o * stride + first : o * stride + first + count].bitcast(FP8X4),
+                rhs_scale=moving_planes[4 * o :, first : first + count],
+                start=(o == 0),
+                stop=(o == PASSES - 1),
+            )
+
+        gathered = {}
+
+        def slots_of(e):
+            g, first = divmod(e * C, GATHER)
+            if g not in gathered:
+                gathered.setdefault(g, gather_tokens(g))
+            return gathered[g] + (GATHER, first, C)
+
+        def routed_run(experts, halves, loader):
+            width = len(halves) * P
+            accs = [psum.tile([P, len(experts) * C], F32, name="acc", bufs=4) for h in halves]
+            for n, e in enumerate(experts):
+                codes, scales = quantize(loader(e), width, width * 1 // 4)
+                slots = slots_of(e)
+                if len(experts) == 1:
+                    order = [(i, o) for o in range(PASSES) for i in range(len(halves))]
+                else:
+                    order = [(i, o) for i in range(len(halves)) for o in range(PASSES)]
+                for i, o in order:
+                    one_pass(accs[i][:, n * C : (n + 1) * C], o, codes, scales, width, i, *slots)
+            return accs
+
+        def add_bias(experts, halves, accs):
+            e0, count = experts[0], len(experts)
+            for acc, h in zip(accs, halves):
+                dst = y[h][:, e0 * C : (e0 + count) * C]
+                if count == 1:
+                    nc.vector.tensor_scalar(out=dst, in0=acc[:], scalar1=bias[:, h, e0 : e0 + 1], scalar2=None, op0=ADD)
+                else:
+                    nc.vector.tensor_tensor(
+                        out=dst.rearrange("p (e c) -> p e c", c=C),
+                        in0=acc[:].rearrange("p (e c) -> p e c", c=C),
+                        in1=bias[:, h, e0 : e0 + count].unsqueeze(2).to_broadcast([P, count, C]),
+                        op=ADD,
+                    )
+
+        def shared(raws):
+            codes, scales = quantize(raws, N, N)
+            for h in range(HALVES):
+                for first, count in ((0, 512), (512, T - 512)):
+                    acc = psum.tile([P, count], F32, name="acc", bufs=4)
+                    for o in range(PASSES):
+                        one_pass(acc[:], o, codes, scales, N, h, words, planes, T, first, count)
+                    nc.scalar.activation(
+                        out=ys[h][:, first : first + count], in_=acc[:], func=IDENTITY, bias=bias[:, h, SHARED : SHARED + 1]
+                    )
+
+        def spread_gate():
+            turned = psum.tile([P, P], F32, name="turned")
+            nc.tensor.transpose(turned[:], gate_rows[:], ident[:])
+            rows = TOP * T // P
+            nc.scalar.copy(out=gate_cols[:, :rows], in_=turned[:, :rows])
+            for first in range(0, rows, 4):
+                back = psum.tile([P, 4 * P], F32, name="back")
+                for i in range(4):
+                    column = gate_cols[:, first + i : first + i + 1].to_broadcast([P, P])
+                    nc.tensor.transpose(back[:, i * P : (i + 1) * P], column, ident[:])
+                nc.scalar.copy(out=gate_sb[:, first * P : (first + 4) * P], in_=back[:])
+
+        def weigh(h, t0, count):
+            products = ring.tile([P, TOP * count], F32, name="products", bufs=6)
+            for r in range(TOP):
+                nc.vector.tensor_tensor(
+                    out=products[:, r * count : (r + 1) * count],
+                    in0=y[h][:].indirect(pos_sb[r][:, t0 // 16 : (t0 + count) // 16]),
+                    in1=gate_sb[:, r * T + t0 : r * T + t0 + count],
+                    op=MULT,
+                )
+            return products
+
+        def add_up(h, t0, count, products):
+            turned = psum.tile([P, count], F32, name="turned")
+            for c in range(0, count, P):
+                terms = [products[:, r * count + c : r * count + c + P] for r in range(TOP)]
+                shared_term = [ys[h][:, t0 + c : t0 + c + P]]
+                terms = terms + shared_term if h == 0 else shared_term + terms
+                for i, term in enumerate(terms):
+                    nc.tensor.matmul(
+                        turned[:, c : c + P], lhsT=term, rhs=ident[:], is_transpose=True,
+                        start=(i == 0), stop=(i == len(terms) - 1),
+                    )
+            total = ring.tile([P, count], F32, name="total")
+            nc.scalar.copy(out=total[:], in_=turned[:])
+            back = psum.tile([P, count], F32, name="back")
+            for c in range(0, count, P):
+                nc.tensor.transpose(back[:, c : c + P], total[:, c : c + P], ident[:])
+            result = ring.tile([P, count], F32, name="result", bufs=3)
+            nc.scalar.copy(out=result[:], in_=back[:])
+            nc.sync.dma_start(out=out[h * P : (h + 1) * P, t0 : t0 + count], in_=result[:])
+
+        def finish_on_vector(h, t0, count):
+            products = ring.tile([P, TOP * count], F32, name="products", bufs=6)
+            sums = ring.tile([P, TOP * count], F32, name="sums", bufs=1)
+            total = ys[h][:, t0 : t0 + count]
+            for r in range(TOP + 1):
+                if r < TOP:
+                    nc.vector.tensor_tensor(
+                        out=products[:, r * count : (r + 1) * count],
+                        in0=y[h][:].indirect(pos_sb[r][:, t0 // 16 : (t0 + count) // 16]),
+                        in1=gate_sb[:, r * T + t0 : r * T + t0 + count],
+                        op=MULT,
+                    )
+                if r > 0:
+                    cols = slice((r - 1) * count, r * count)
+                    nc.vector.tensor_tensor(out=sums[:, cols], in0=total, in1=products[:, cols], op=ADD)
+                    total = sums[:, cols]
+            nc.sync.dma_start(out=out[h * P : (h + 1) * P, t0 : t0 + count], in_=total)
+
+        both = tuple(range(HALVES))
+        for q in range(4):
+            nc.scalar.dma_start(
+                out=planes[32 * q : 32 * q + 4 * PASSES, :T].bitcast(I32),
+                in_=x_scales[:, 4 * q : 4 * q + 4, :].bitcast(I32),
+            )
+        nc.scalar.dma_start(out=gate_rows[: TOP * T // P, :], in_=gate[:, 0, :].rearrange("r (c t) -> r c t", t=P))
+        nc.scalar.dma_start(out=bias[:, :, : E + 1], in_=b.rearrange("(h p) e -> p h e", p=P))
+
+        nc.sync.dma_start(out=offs_sb[:], in_=offs)
+        nc.sync.dma_start(
+            out=words[:, : PASSES * T].rearrange("p (o t) -> p o t", t=T),
+            in_=x_words.rearrange("o p t r -> p o (t r)").bitcast(I32),
+        )
+
+        def load(e):
+            if e == 3:
+                for r, pos in enumerate((pos1, pos2, pos3, pos4)):
+                    nc.sync.dma_start(out=pos_sb[r][:], in_=pos)
+            if e == 0 or e == E - 1:
+                return [load_pass(e, o, both) for o in range(PASSES)]
+            return load_whole(e)
+
+        spread_gate()
+        runs = [tuple(range(e, e + 4)) for e in range(0, 16, 4)] + [(16, 17, 18), (19,)]
+        for experts in runs:
+            accs = routed_run(experts, both, load)
+            add_bias(experts, both, accs)
+        shared_raws = [load_pass(SHARED, o, both) for o in range(PASSES)]
+        early = [weigh(0, t0, count) for t0, count in TOKEN_CHUNKS[:2]]
+        shared(shared_raws)
+        early.extend([weigh(0, t0, count) for t0, count in TOKEN_CHUNKS[2:]])
+        for (t0, count), products in zip(TOKEN_CHUNKS, early):
+            add_up(0, t0, count, products)
+        for t0, count in TOKEN_CHUNKS[:-1]:
+            add_up(1, t0, count, weigh(1, t0, count))
+        finish_on_vector(1, *TOKEN_CHUNKS[-1])

@@ -50,7 +50,7 @@ def tile_moe_shr_lin_bias_kernel(
         gate_sb = keep.tile([P, TOP * T], F32, name="gate_sb")
         ident = keep.tile([P, P], F32, name="ident")
         y = [keep.tile([P, SLOTS], F32, name="y%d" % h) for h in range(HALVES)]
-        ys = [keep.tile([P, T], F32, name="ys%d" % h) for h in range(HALVES)]
+        ys_turned = [keep.tile([P, N], F32, name="ys_turned%d" % c) for c in range(T // P)]
 
         nc.vector.memset(planes[:].bitcast(I32), 0)
         nc.vector.memset(words[:, PASSES * T :], 0)
@@ -64,7 +64,7 @@ def tile_moe_shr_lin_bias_kernel(
 
         def load_pass(e, o, halves):
             width = len(halves) * P
-            raw_pass = ring.tile([P, PACK, width], F32, name="raw_pass", bufs=6)
+            raw_pass = ring.tile([P, PACK, width], F32, name="raw_pass%d" % width, bufs=6 if width == N else 1)
             rows = w[e, o * P * PACK : (o + 1) * P * PACK, halves[0] * P : halves[0] * P + width]
             nc.sync.dma_start(out=raw_pass[:], in_=rows.rearrange("(p j) n -> p j n", j=PACK))
             return raw_pass[:]
@@ -122,11 +122,11 @@ def tile_moe_shr_lin_bias_kernel(
                 gathered.setdefault(g, gather_tokens(g))
             return gathered[g] + (GATHER, first, C)
 
-        def routed_run(experts, halves, loader):
+        def routed_run(experts, halves, loader, scalar_share):
             width = len(halves) * P
             accs = [psum.tile([P, len(experts) * C], F32, name="acc", bufs=4) for h in halves]
             for n, e in enumerate(experts):
-                codes, scales = quantize(loader(e), width, width * 1 // 4)
+                codes, scales = quantize(loader(e), width, width * scalar_share // 8)
                 slots = slots_of(e)
                 if len(experts) == 1:
                     order = [(i, o) for o in range(PASSES) for i in range(len(halves))]
@@ -152,14 +152,33 @@ def tile_moe_shr_lin_bias_kernel(
 
         def shared(raws):
             codes, scales = quantize(raws, N, N)
-            for h in range(HALVES):
-                for first, count in ((0, 512), (512, T - 512)):
-                    acc = psum.tile([P, count], F32, name="acc", bufs=4)
-                    for o in range(PASSES):
-                        one_pass(acc[:], o, codes, scales, N, h, words, planes, T, first, count)
-                    nc.scalar.activation(
-                        out=ys[h][:, first : first + count], in_=acc[:], func=IDENTITY, bias=bias[:, h, SHARED : SHARED + 1]
-                    )
+
+            def turned_pass(acc, o, c, count):
+                nc.tensor.matmul_mx(
+                    out=acc,
+                    lhsT=words[:, o * T + c * P : o * T + (c + 1) * P].bitcast(FP8X4),
+                    lhsT_scale=planes[4 * o :, c * P : (c + 1) * P],
+                    rhs=codes[:, o * N : o * N + count].bitcast(FP8X4),
+                    rhs_scale=scales[:, o * N : o * N + count],
+                    start=(o == 0),
+                    stop=(o == PASSES - 1),
+                )
+
+            last = T // P - 1
+            accs = [psum.tile([P, N], F32, name="acc", bufs=4) for c in range(last)]
+            for o in range(PASSES):
+                for c in range(last):
+                    turned_pass(accs[c][:], o, c, N)
+                    if o == PASSES - 1:
+                        nc.scalar.copy(out=ys_turned[c][:], in_=accs[c][:])
+            acc = psum.tile([P, P], F32, name="acc", bufs=4)
+            for o in range(PASSES):
+                turned_pass(acc[:], o, last, P)
+            nc.scalar.copy(out=ys_turned[last][:, :P], in_=acc[:])
+            ys_last = psum.tile([P, P], F32, name="acc", bufs=4)
+            for o in range(PASSES):
+                one_pass(ys_last[:], o, codes, scales, N, 1, words, planes, T, last * P, P)
+            return ys_last
 
         def spread_gate():
             turned = psum.tile([P, P], F32, name="turned")
@@ -174,7 +193,7 @@ def tile_moe_shr_lin_bias_kernel(
                 nc.scalar.copy(out=gate_sb[:, first * P : (first + 4) * P], in_=back[:])
 
         def weigh(h, t0, count):
-            products = ring.tile([P, TOP * count], F32, name="products", bufs=6)
+            products = keep.tile([P, TOP * count], F32, name="products%d_%d" % (h, t0))
             for r in range(TOP):
                 nc.vector.tensor_tensor(
                     out=products[:, r * count : (r + 1) * count],
@@ -184,30 +203,35 @@ def tile_moe_shr_lin_bias_kernel(
                 )
             return products
 
-        def add_up(h, t0, count, products):
-            turned = psum.tile([P, count], F32, name="turned")
+        def add_turned(count, products):
+            totals = []
             for c in range(0, count, P):
-                terms = [products[:, r * count + c : r * count + c + P] for r in range(TOP)]
-                shared_term = [ys[h][:, t0 + c : t0 + c + P]]
-                terms = terms + shared_term if h == 0 else shared_term + terms
-                for i, term in enumerate(terms):
+                turned = psum.tile([P, P], F32, name="turned")
+                for r in range(TOP):
                     nc.tensor.matmul(
-                        turned[:, c : c + P], lhsT=term, rhs=ident[:], is_transpose=True,
-                        start=(i == 0), stop=(i == len(terms) - 1),
+                        turned[:], lhsT=products[:, r * count + c : r * count + c + P], rhs=ident[:],
+                        is_transpose=True, start=(r == 0), stop=(r == TOP - 1),
                     )
-            total = ring.tile([P, count], F32, name="total")
-            nc.scalar.copy(out=total[:], in_=turned[:])
-            back = psum.tile([P, count], F32, name="back")
-            for c in range(0, count, P):
-                nc.tensor.transpose(back[:, c : c + P], total[:, c : c + P], ident[:])
-            result = ring.tile([P, count], F32, name="result", bufs=3)
-            nc.scalar.copy(out=result[:], in_=back[:])
-            nc.sync.dma_start(out=out[h * P : (h + 1) * P, t0 : t0 + count], in_=result[:])
+                total = ring.tile([P, P], F32, name="total", bufs=2 * T // P)
+                nc.scalar.copy(out=total[:], in_=turned[:])
+                totals.append(total)
+            return totals
 
-        def finish_on_vector(h, t0, count):
-            products = ring.tile([P, TOP * count], F32, name="products", bufs=6)
+        def turn_back(h, t0, count, totals):
+            result = keep.tile([P, count], F32, name="result%d_%d" % (h, t0))
+            for c, total in enumerate(totals):
+                back = psum.tile([P, P], F32, name="back")
+                terms = (ys_turned[t0 // P + c][:, h * P : (h + 1) * P], total[:])
+                for i, term in enumerate(terms):
+                    nc.tensor.matmul(back[:], lhsT=term, rhs=ident[:], is_transpose=True, start=(i == 0), stop=(i == 1))
+                nc.scalar.activation(
+                    out=result[:, c * P : (c + 1) * P], in_=back[:], func=IDENTITY, bias=bias[:, h, SHARED : SHARED + 1]
+                )
+            nc.scalar.dma_start(out=out[h * P : (h + 1) * P, t0 : t0 + count], in_=result[:])
+
+        def finish_on_vector(h, t0, count, ys_last):
+            products = keep.tile([P, TOP * count], F32, name="products_last")
             sums = ring.tile([P, TOP * count], F32, name="sums", bufs=1)
-            total = ys[h][:, t0 : t0 + count]
             for r in range(TOP + 1):
                 if r < TOP:
                     nc.vector.tensor_tensor(
@@ -218,9 +242,15 @@ def tile_moe_shr_lin_bias_kernel(
                     )
                 if r > 0:
                     cols = slice((r - 1) * count, r * count)
-                    nc.vector.tensor_tensor(out=sums[:, cols], in0=total, in1=products[:, cols], op=ADD)
-                    total = sums[:, cols]
-            nc.sync.dma_start(out=out[h * P : (h + 1) * P, t0 : t0 + count], in_=total)
+                    if r == 1:
+                        nc.vector.scalar_tensor_tensor(
+                            out=sums[:, cols], in0=ys_last[:], scalar=bias[:, h, SHARED : SHARED + 1],
+                            in1=products[:, cols], op0=ADD, op1=ADD,
+                        )
+                    else:
+                        before = sums[:, (r - 2) * count : (r - 1) * count]
+                        nc.vector.tensor_tensor(out=sums[:, cols], in0=before, in1=products[:, cols], op=ADD)
+            nc.sync.dma_start(out=out[h * P : (h + 1) * P, t0 : t0 + count], in_=sums[:, (TOP - 1) * count :])
 
         both = tuple(range(HALVES))
         for q in range(4):
@@ -246,16 +276,12 @@ def tile_moe_shr_lin_bias_kernel(
             return load_whole(e)
 
         spread_gate()
-        runs = [tuple(range(e, e + 4)) for e in range(0, 16, 4)] + [(16, 17, 18), (19,)]
-        for experts in runs:
-            accs = routed_run(experts, both, load)
-            add_bias(experts, both, accs)
+        routed = ((0, 1, 2, 3), (4, 5, 6, 7), (8, 9, 10, 11), (12, 13, 14, 15), (16, 17, 18), (19,))
+        for experts in routed:
+            add_bias(experts, both, routed_run(experts, both, load, 2))
         shared_raws = [load_pass(SHARED, o, both) for o in range(PASSES)]
-        early = [weigh(0, t0, count) for t0, count in TOKEN_CHUNKS[:2]]
-        shared(shared_raws)
-        early.extend([weigh(0, t0, count) for t0, count in TOKEN_CHUNKS[2:]])
-        for (t0, count), products in zip(TOKEN_CHUNKS, early):
-            add_up(0, t0, count, products)
+        ys_last = shared(shared_raws)
+        turn_back(0, 0, T, add_turned(T, weigh(0, 0, T)))
         for t0, count in TOKEN_CHUNKS[:-1]:
-            add_up(1, t0, count, weigh(1, t0, count))
-        finish_on_vector(1, *TOKEN_CHUNKS[-1])
+            turn_back(1, t0, count, add_turned(count, weigh(1, t0, count)))
+        finish_on_vector(1, *TOKEN_CHUNKS[-1], ys_last)

@@ -28,6 +28,8 @@ SHARED = E
 GATHER = 512
 WINDOW = 704
 SPLIT = 0
+LANDING_BYTES = 7 * 4 * PASSES * PACK * N
+WHOLE_SCALAR_COLS = 208
 TOKEN_CHUNKS = ((0, 256), (256, 256), (512, 128))
 
 
@@ -38,11 +40,12 @@ def tile_moe_shr_lin_bias_kernel(
     with ExitStack() as ctx:
         keep = ctx.enter_context(tc.tile_pool(name="keep", bufs=1))
         ring = ctx.enter_context(tc.tile_pool(name="ring", bufs=2))
+        landing = ctx.enter_context(tc.tile_pool(name="landing", bufs=1))
         psum = ctx.enter_context(tc.psum_pool(name="psum", bufs=2))
 
         offs_sb = keep.tile([P, SLOTS // 16], U16, name="offs_sb")
         pos_sb = [keep.tile([P, T // 16], U16, name="pos_sb%d" % r) for r in range(TOP)]
-        words = keep.tile([P, (PASSES - 1) * T + WINDOW], I32, name="words", align_bytes=64)
+        words = [keep.tile([P, WINDOW], I32, name="words%d" % o, align_bytes=64) for o in range(PASSES)]
         planes = keep.tile([P, WINDOW], U8, name="planes", align_bytes=64)
         bias = keep.tile([P, HALVES, 24], F32, name="bias")
         gate_rows = keep.tile([P, P], F32, name="gate_rows")
@@ -50,24 +53,33 @@ def tile_moe_shr_lin_bias_kernel(
         gate_sb = keep.tile([P, TOP * T], F32, name="gate_sb")
         ident = keep.tile([P, P], F32, name="ident")
         y = [keep.tile([P, SLOTS], F32, name="y%d" % h) for h in range(HALVES)]
-        ys_turned = [keep.tile([P, N], F32, name="ys_turned%d" % c) for c in range(T // P)]
+        ys_turned = []
 
         nc.vector.memset(planes[:].bitcast(I32), 0)
-        nc.vector.memset(words[:, PASSES * T :], 0)
+        for o in range(PASSES):
+            nc.vector.memset(words[o][:, T:], 0)
         nc.gpsimd.memset(gate_rows[:], 0.0)
         make_identity(nc, ident[:])
 
+        landed = [0]
+
+        def landing_tile(shape, name):
+            size = 4 * shape[1] * shape[2]
+            start = landed[-1] if landed[-1] + size <= LANDING_BYTES else 0
+            landed.append(start + size)
+            return landing.tile(shape, F32, name=name, offset=start)
+
         def load_whole(e):
-            raw = ring.tile([P, PASSES, PACK * N], F32, name="raw", bufs=5)
+            raw = landing_tile([P, PASSES, PACK * N], "raw%d" % e)
             nc.sync.dma_start(out=raw[:], in_=w[e].rearrange("(o p j) n -> p o (j n)", p=P, j=PACK))
-            return [raw[:, o, :].rearrange("p (j n) -> p j n", j=PACK) for o in range(PASSES)]
+            return raw[:].rearrange("p o (j n) -> p o j n", j=PACK)
 
         def load_pass(e, o, halves):
             width = len(halves) * P
-            raw_pass = ring.tile([P, PACK, width], F32, name="raw_pass%d" % width, bufs=6 if width == N else 1)
+            raw = landing_tile([P, PACK, width], "raw%d_%d_%d" % (e, o, halves[0]))
             rows = w[e, o * P * PACK : (o + 1) * P * PACK, halves[0] * P : halves[0] * P + width]
-            nc.sync.dma_start(out=raw_pass[:], in_=rows.rearrange("(p j) n -> p j n", j=PACK))
-            return raw_pass[:]
+            nc.sync.dma_start(out=raw[:], in_=rows.rearrange("(p j) n -> p j n", j=PACK))
+            return raw[:]
 
         def cast(engine, dst, src):
             dst = dst.rearrange("p (c i j) -> p c j i", i=4, j=PACK)
@@ -78,37 +90,43 @@ def tile_moe_shr_lin_bias_kernel(
                 nc.vector.tensor_copy(out=dst, in_=src)
 
         def quantize(raws, width, scalar_cols):
-            codes = ring.tile([P, PASSES * width], U32, name="codes", bufs=4, align_bytes=64)
-            scales = ring.tile([P, PASSES * width], U8, name="scales", bufs=4, align_bytes=64)
-            front = ring.tile([P, 2 * PACK * width], BF16, name="front", bufs=4, align_bytes=64)
-            last = ring.tile([P, PACK * width], BF16, name="last", bufs=4, align_bytes=64)
-            for o in range(2):
-                cast("S", front[:, o * PACK * width : (o + 1) * PACK * width], raws[o])
-            if scalar_cols > 0:
+            codes = ring.tile([P, PASSES * width], U32, name="codes", bufs=6, align_bytes=64)
+            scales = ring.tile([P, PASSES * width], U8, name="scales", bufs=6, align_bytes=64)
+            stage = ring.tile([P, PASSES * PACK * width], BF16, name="stage", bufs=4, align_bytes=64)
+            front, last = stage[:, : 2 * PACK * width], stage[:, 2 * PACK * width :]
+            if isinstance(raws, list):
+                for o in range(2):
+                    cast("S", front[:, o * PACK * width : (o + 1) * PACK * width], raws[o])
                 cast("S", last[:, : PACK * scalar_cols], raws[2][:, :, :scalar_cols])
-            if scalar_cols < width:
-                cast("V", last[:, PACK * scalar_cols :], raws[2][:, :, scalar_cols:])
-            nc.vector.quantize_mx(out=codes[:, : 2 * width].bitcast(FP8X4), scales=scales[:, : 2 * width], in_=front[:])
-            nc.vector.quantize_mx(out=codes[:, 2 * width :].bitcast(FP8X4), scales=scales[:, 2 * width :], in_=last[:])
+                if scalar_cols < width:
+                    cast("V", last[:, PACK * scalar_cols :], raws[2][:, :, scalar_cols:])
+            else:
+                dst = stage[:].rearrange("p (o c i j) -> p c o j i", o=PASSES, i=4, j=PACK)
+                src = raws.rearrange("p o j (c i) -> p c o j i", i=4)
+                cut = WHOLE_SCALAR_COLS // 4
+                nc.scalar.copy(out=dst[:, :cut], in_=src[:, :cut])
+                nc.vector.tensor_copy(out=dst[:, cut:], in_=src[:, cut:])
+            nc.vector.quantize_mx(out=codes[:, : 2 * width].bitcast(FP8X4), scales=scales[:, : 2 * width], in_=front)
+            nc.vector.quantize_mx(out=codes[:, 2 * width :].bitcast(FP8X4), scales=scales[:, 2 * width :], in_=last)
             return codes, scales
 
         def gather_tokens(g):
             slot_words = ring.tile([P, PASSES * GATHER], U32, name="slot_words", align_bytes=64)
             slot_planes = ring.tile([P, GATHER], U8, name="slot_planes", align_bytes=64)
             entries = offs_sb[:, g * GATHER // 16 : (g + 1) * GATHER // 16]
-            nc.vector.tensor_copy(out=slot_planes[:], in_=planes[:].indirect(entries))
             for o in range(PASSES):
-                window = words[:, o * T : o * T + WINDOW].bitcast(U32)
+                window = words[o][:].bitcast(U32)
                 nc.vector.tensor_copy(out=slot_words[:, o * GATHER : (o + 1) * GATHER], in_=window.indirect(entries))
-            return slot_words, slot_planes
+            nc.vector.tensor_copy(out=slot_planes[:], in_=planes[:].indirect(entries))
+            return [slot_words[:, o * GATHER : (o + 1) * GATHER] for o in range(PASSES)], slot_planes
 
-        def one_pass(acc, o, codes, scales, width, i, moving, moving_planes, stride, first, count):
+        def one_pass(acc, o, codes, scales, width, i, moving, moving_planes, first, count):
             cols = slice(o * width + i * P, o * width + (i + 1) * P)
             nc.tensor.matmul_mx(
                 out=acc,
                 lhsT=codes[:, cols].bitcast(FP8X4),
                 lhsT_scale=scales[:, cols],
-                rhs=moving[:, o * stride + first : o * stride + first + count].bitcast(FP8X4),
+                rhs=moving[o][:, first : first + count].bitcast(FP8X4),
                 rhs_scale=moving_planes[4 * o :, first : first + count],
                 start=(o == 0),
                 stop=(o == PASSES - 1),
@@ -120,13 +138,13 @@ def tile_moe_shr_lin_bias_kernel(
             g, first = divmod(e * C, GATHER)
             if g not in gathered:
                 gathered.setdefault(g, gather_tokens(g))
-            return gathered[g] + (GATHER, first, C)
+            return gathered[g] + (first, C)
 
         def routed_run(experts, halves, loader, scalar_share):
             width = len(halves) * P
             accs = [psum.tile([P, len(experts) * C], F32, name="acc", bufs=4) for h in halves]
             for n, e in enumerate(experts):
-                codes, scales = quantize(loader(e), width, width * scalar_share // 8)
+                codes, scales = quantize(loader(e), width, width * scalar_share // 16)
                 slots = slots_of(e)
                 if len(experts) == 1:
                     order = [(i, o) for o in range(PASSES) for i in range(len(halves))]
@@ -156,7 +174,7 @@ def tile_moe_shr_lin_bias_kernel(
             def turned_pass(acc, o, c, count):
                 nc.tensor.matmul_mx(
                     out=acc,
-                    lhsT=words[:, o * T + c * P : o * T + (c + 1) * P].bitcast(FP8X4),
+                    lhsT=words[o][:, c * P : (c + 1) * P].bitcast(FP8X4),
                     lhsT_scale=planes[4 * o :, c * P : (c + 1) * P],
                     rhs=codes[:, o * N : o * N + count].bitcast(FP8X4),
                     rhs_scale=scales[:, o * N : o * N + count],
@@ -165,20 +183,23 @@ def tile_moe_shr_lin_bias_kernel(
                 )
 
             last = T // P - 1
-            accs = [psum.tile([P, N], F32, name="acc", bufs=4) for c in range(last)]
+            accs = [psum.tile([P, N], F32, name=("turned", "back")[c % 2]) for c in range(last)]
             for o in range(PASSES):
                 for c in range(last):
                     turned_pass(accs[c][:], o, c, N)
-                    if o == PASSES - 1:
-                        nc.scalar.copy(out=ys_turned[c][:], in_=accs[c][:])
             acc = psum.tile([P, P], F32, name="acc", bufs=4)
             for o in range(PASSES):
                 turned_pass(acc[:], o, last, P)
-            nc.scalar.copy(out=ys_turned[last][:, :P], in_=acc[:])
             ys_last = psum.tile([P, P], F32, name="acc", bufs=4)
             for o in range(PASSES):
-                one_pass(ys_last[:], o, codes, scales, N, 1, words, planes, T, last * P, P)
-            return ys_last
+                one_pass(ys_last[:], o, codes, scales, N, 1, words, planes, last * P, P)
+            return accs + [acc], ys_last
+
+        def keep_shared(accs):
+            start = landed[-1] - 4 * PASSES * PACK * P
+            for c, acc in enumerate(accs):
+                ys_turned.append(landing.tile([P, N], F32, name="ys_turned%d" % c, offset=start + 4 * N * c))
+                nc.scalar.copy(out=ys_turned[c][:, : acc.shape[1]], in_=acc[:])
 
         def spread_gate():
             turned = psum.tile([P, P], F32, name="turned")
@@ -262,10 +283,8 @@ def tile_moe_shr_lin_bias_kernel(
         nc.scalar.dma_start(out=bias[:, :, : E + 1], in_=b.rearrange("(h p) e -> p h e", p=P))
 
         nc.sync.dma_start(out=offs_sb[:], in_=offs)
-        nc.sync.dma_start(
-            out=words[:, : PASSES * T].rearrange("p (o t) -> p o t", t=T),
-            in_=x_words.rearrange("o p t r -> p o (t r)").bitcast(I32),
-        )
+        for o in range(PASSES):
+            nc.sync.dma_start(out=words[o][:, :T], in_=x_words[o].rearrange("p t r -> p (t r)").bitcast(I32))
 
         def load(e):
             if e == 3:
@@ -276,12 +295,18 @@ def tile_moe_shr_lin_bias_kernel(
             return load_whole(e)
 
         spread_gate()
-        routed = ((0, 1, 2, 3), (4, 5, 6, 7), (8, 9, 10, 11), (12, 13, 14, 15), (16, 17, 18), (19,))
-        for experts in routed:
-            add_bias(experts, both, routed_run(experts, both, load, 2))
-        shared_raws = [load_pass(SHARED, o, both) for o in range(PASSES)]
-        ys_last = shared(shared_raws)
-        turn_back(0, 0, T, add_turned(T, weigh(0, 0, T)))
+        for experts in ((0, 1, 2, 3), (4, 5, 6, 7), (8, 9, 10, 11), (12, 13, 14, 15)):
+            add_bias(experts, both, routed_run(experts, both, load, 7))
+        for experts in ((16, 17, 18), (19,)):
+            accs = routed_run(experts, (0,), lambda e: [load_pass(e, o, (0,)) for o in range(PASSES)], 7)
+            add_bias(experts, (0,), accs)
+        shared_accs, ys_last = shared([load_pass(SHARED, o, both) for o in range(PASSES)])
+        first_products = weigh(0, 0, T)
+        for experts in ((16, 17, 18), (19,)):
+            accs = routed_run(experts, (1,), lambda e: [load_pass(e, o, (1,)) for o in range(PASSES)], 16)
+            add_bias(experts, (1,), accs)
+        keep_shared(shared_accs)
+        turn_back(0, 0, T, add_turned(T, first_products))
         for t0, count in TOKEN_CHUNKS[:-1]:
             turn_back(1, t0, count, add_turned(count, weigh(1, t0, count)))
         finish_on_vector(1, *TOKEN_CHUNKS[-1], ys_last)

@@ -27,10 +27,11 @@ SLOTS = E * C
 SHARED = E
 GATHER = 512
 WINDOW = 704
-SPLIT = 0
-LANDING_BYTES = 7 * 4 * PASSES * PACK * N
-WHOLE_SCALAR_COLS = 208
-TOKEN_CHUNKS = ((0, 256), (256, 256), (512, 128))
+EXPERT_BYTES = 4 * PASSES * PACK * N
+LANDING_BYTES = 7 * EXPERT_BYTES
+WHOLE_SCALAR_COLS = 200
+SHARED_AFTER = 8
+UNITS = ((0, 0, 256), (0, 256, 256), (0, 512, 128), (1, 0, 256), (1, 256, 128), (1, 384, 128))
 
 
 def tile_moe_shr_lin_bias_kernel(
@@ -49,16 +50,16 @@ def tile_moe_shr_lin_bias_kernel(
         planes = keep.tile([P, WINDOW], U8, name="planes", align_bytes=64)
         bias = keep.tile([P, HALVES, 24], F32, name="bias")
         gate_rows = keep.tile([P, P], F32, name="gate_rows")
-        gate_cols = keep.tile([P, 24], F32, name="gate_cols")
+        gate_cols = keep.tile([P, P], F32, name="gate_cols")
         gate_sb = keep.tile([P, TOP * T], F32, name="gate_sb")
         ident = keep.tile([P, P], F32, name="ident")
         y = [keep.tile([P, SLOTS], F32, name="y%d" % h) for h in range(HALVES)]
-        ys_turned = []
+        ys_turned = keep.tile([P, T // P, N], F32, name="ys_turned")
+        ys_last = keep.tile([P, P], F32, name="ys_last")
 
         nc.vector.memset(planes[:].bitcast(I32), 0)
         for o in range(PASSES):
             nc.vector.memset(words[o][:, T:], 0)
-        nc.gpsimd.memset(gate_rows[:], 0.0)
         make_identity(nc, ident[:])
 
         landed = [0]
@@ -74,40 +75,63 @@ def tile_moe_shr_lin_bias_kernel(
             nc.sync.dma_start(out=raw[:], in_=w[e].rearrange("(o p j) n -> p o (j n)", p=P, j=PACK))
             return raw[:].rearrange("p o (j n) -> p o j n", j=PACK)
 
-        def load_pass(e, o, halves):
-            width = len(halves) * P
-            raw = landing_tile([P, PACK, width], "raw%d_%d_%d" % (e, o, halves[0]))
-            rows = w[e, o * P * PACK : (o + 1) * P * PACK, halves[0] * P : halves[0] * P + width]
+        def load_pass(e, o, first, width):
+            raw = landing_tile([P, PACK, width], "raw%d_%d_%d" % (e, first, o))
+            rows = w[e, o * P * PACK : (o + 1) * P * PACK, first : first + width]
             nc.sync.dma_start(out=raw[:], in_=rows.rearrange("(p j) n -> p j n", j=PACK))
             return raw[:]
 
-        def cast(engine, dst, src):
-            dst = dst.rearrange("p (c i j) -> p c j i", i=4, j=PACK)
-            src = src.rearrange("p j (c i) -> p c j i", i=4)
-            if engine == "S":
-                nc.scalar.activation(out=dst, in_=src, func=COPY)
-            else:
-                nc.vector.tensor_copy(out=dst, in_=src)
-
-        def quantize(raws, width, scalar_cols):
+        def mx_tiles(width):
             codes = ring.tile([P, PASSES * width], U32, name="codes", bufs=6, align_bytes=64)
             scales = ring.tile([P, PASSES * width], U8, name="scales", bufs=6, align_bytes=64)
             stage = ring.tile([P, PASSES * PACK * width], BF16, name="stage", bufs=4, align_bytes=64)
-            front, last = stage[:, : 2 * PACK * width], stage[:, 2 * PACK * width :]
-            if isinstance(raws, list):
-                for o in range(2):
-                    cast("S", front[:, o * PACK * width : (o + 1) * PACK * width], raws[o])
-                cast("S", last[:, : PACK * scalar_cols], raws[2][:, :, :scalar_cols])
-                if scalar_cols < width:
-                    cast("V", last[:, PACK * scalar_cols :], raws[2][:, :, scalar_cols:])
-            else:
-                dst = stage[:].rearrange("p (o c i j) -> p c o j i", o=PASSES, i=4, j=PACK)
-                src = raws.rearrange("p o j (c i) -> p c o j i", i=4)
-                cut = WHOLE_SCALAR_COLS // 4
-                nc.scalar.copy(out=dst[:, :cut], in_=src[:, :cut])
-                nc.vector.tensor_copy(out=dst[:, cut:], in_=src[:, cut:])
-            nc.vector.quantize_mx(out=codes[:, : 2 * width].bitcast(FP8X4), scales=scales[:, : 2 * width], in_=front)
-            nc.vector.quantize_mx(out=codes[:, 2 * width :].bitcast(FP8X4), scales=scales[:, 2 * width :], in_=last)
+            return codes, scales, stage
+
+        def quantize(codes, scales, stage, width):
+            for a, z in ((0, 2 * width), (2 * width, 3 * width)):
+                nc.vector.quantize_mx(
+                    out=codes[:, a:z].bitcast(FP8X4), scales=scales[:, a:z], in_=stage[:, PACK * a : PACK * z]
+                )
+            return codes, scales
+
+        def whole_expert(e):
+            raws = load_whole(e)
+            codes, scales, stage = mx_tiles(N)
+            dst = stage[:].rearrange("p (o c i j) -> p c o j i", o=PASSES, i=4, j=PACK)
+            src = raws.rearrange("p o j (c i) -> p c o j i", i=4)
+            cut = WHOLE_SCALAR_COLS // 4
+            nc.scalar.copy(out=dst[:, :cut], in_=src[:, :cut])
+            nc.vector.tensor_copy(out=dst[:, cut:], in_=src[:, cut:])
+            return quantize(codes, scales, stage, N)
+
+        def expert_by_pass(e, first, width, scalar_passes):
+            raws = [load_pass(e, o, first, width) for o in range(PASSES)]
+            codes, scales, stage = mx_tiles(width)
+            for o in range(PASSES):
+                dst = stage[:, o * PACK * width : (o + 1) * PACK * width]
+                dst = dst.rearrange("p (c i j) -> p c j i", i=4, j=PACK)
+                src = raws[o].rearrange("p j (c i) -> p c j i", i=4)
+                if o < scalar_passes:
+                    nc.scalar.copy(out=dst, in_=src)
+                else:
+                    nc.vector.tensor_copy(out=dst, in_=src)
+            return quantize(codes, scales, stage, width)
+
+        def last_expert(e):
+            raws = [load_pass(e, o, 0, N) for o in range(PASSES)]
+            codes, scales, stage = mx_tiles(N)
+            pieces = [(o * N, N, raws[o]) for o in range(PASSES - 1)]
+            pieces.extend([(2 * N + h * P, P, raws[2][:, :, h * P : (h + 1) * P]) for h in range(HALVES)])
+            for n, (first, width, raw) in enumerate(pieces):
+                flat = stage[:, PACK * first : PACK * (first + width)]
+                dst = flat.rearrange("p (c i j) -> p c j i", i=4, j=PACK)
+                src = raw.rearrange("p j (c i) -> p c j i", i=4)
+                if n == 2:
+                    nc.vector.tensor_copy(out=dst, in_=src)
+                else:
+                    nc.scalar.copy(out=dst, in_=src)
+                cols = slice(first, first + width)
+                nc.vector.quantize_mx(out=codes[:, cols].bitcast(FP8X4), scales=scales[:, cols], in_=flat)
             return codes, scales
 
         def gather_tokens(g):
@@ -120,17 +144,18 @@ def tile_moe_shr_lin_bias_kernel(
             nc.vector.tensor_copy(out=slot_planes[:], in_=planes[:].indirect(entries))
             return [slot_words[:, o * GATHER : (o + 1) * GATHER] for o in range(PASSES)], slot_planes
 
-        def one_pass(acc, o, codes, scales, width, i, moving, moving_planes, first, count):
-            cols = slice(o * width + i * P, o * width + (i + 1) * P)
-            nc.tensor.matmul_mx(
-                out=acc,
-                lhsT=codes[:, cols].bitcast(FP8X4),
-                lhsT_scale=scales[:, cols],
-                rhs=moving[o][:, first : first + count].bitcast(FP8X4),
-                rhs_scale=moving_planes[4 * o :, first : first + count],
-                start=(o == 0),
-                stop=(o == PASSES - 1),
-            )
+        def product(acc, codes, scales, width, i, moving, moving_planes, first, passes=range(PASSES)):
+            for o in passes:
+                cols = slice(o * width + i * P, o * width + (i + 1) * P)
+                nc.tensor.matmul_mx(
+                    out=acc,
+                    lhsT=codes[:, cols].bitcast(FP8X4),
+                    lhsT_scale=scales[:, cols],
+                    rhs=moving[o][:, first : first + P].bitcast(FP8X4),
+                    rhs_scale=moving_planes[4 * o :, first : first + P],
+                    start=(o == 0),
+                    stop=(o == PASSES - 1),
+                )
 
         gathered = {}
 
@@ -138,27 +163,27 @@ def tile_moe_shr_lin_bias_kernel(
             g, first = divmod(e * C, GATHER)
             if g not in gathered:
                 gathered.setdefault(g, gather_tokens(g))
-            return gathered[g] + (first, C)
+            return gathered[g] + (first,)
 
-        def routed_run(experts, halves, loader, scalar_share):
+        def routed_run(experts, halves, prepare):
             width = len(halves) * P
             accs = [psum.tile([P, len(experts) * C], F32, name="acc", bufs=4) for h in halves]
             for n, e in enumerate(experts):
-                codes, scales = quantize(loader(e), width, width * scalar_share // 16)
+                codes, scales = prepare(e)
                 slots = slots_of(e)
                 if len(experts) == 1:
-                    order = [(i, o) for o in range(PASSES) for i in range(len(halves))]
+                    for passes in ((0, 1), (2,)):
+                        for i in range(len(halves)):
+                            product(accs[i][:], codes, scales, width, i, *slots, passes=passes)
                 else:
-                    order = [(i, o) for i in range(len(halves)) for o in range(PASSES)]
-                for i, o in order:
-                    one_pass(accs[i][:, n * C : (n + 1) * C], o, codes, scales, width, i, *slots)
-            return accs
-
-        def add_bias(experts, halves, accs):
+                    for i in range(len(halves)):
+                        product(accs[i][:, n * C : (n + 1) * C], codes, scales, width, i, *slots)
             e0, count = experts[0], len(experts)
             for acc, h in zip(accs, halves):
                 dst = y[h][:, e0 * C : (e0 + count) * C]
-                if count == 1:
+                if count == 1 and h == 1:
+                    nc.scalar.activation(out=dst, in_=acc[:], func=IDENTITY, bias=bias[:, h, e0 : e0 + 1])
+                elif count == 1:
                     nc.vector.tensor_scalar(out=dst, in0=acc[:], scalar1=bias[:, h, e0 : e0 + 1], scalar2=None, op0=ADD)
                 else:
                     nc.vector.tensor_tensor(
@@ -168,145 +193,123 @@ def tile_moe_shr_lin_bias_kernel(
                         op=ADD,
                     )
 
-        def shared(raws):
-            codes, scales = quantize(raws, N, N)
+        def shared_expert():
+            codes, scales = whole_expert(SHARED)
 
-            def turned_pass(acc, o, c, count):
-                nc.tensor.matmul_mx(
-                    out=acc,
-                    lhsT=words[o][:, c * P : (c + 1) * P].bitcast(FP8X4),
-                    lhsT_scale=planes[4 * o :, c * P : (c + 1) * P],
-                    rhs=codes[:, o * N : o * N + count].bitcast(FP8X4),
-                    rhs_scale=scales[:, o * N : o * N + count],
-                    start=(o == 0),
-                    stop=(o == PASSES - 1),
-                )
+            def turned_product(acc, c, count):
+                for o in range(PASSES):
+                    nc.tensor.matmul_mx(
+                        out=acc,
+                        lhsT=words[o][:, c * P : (c + 1) * P].bitcast(FP8X4),
+                        lhsT_scale=planes[4 * o :, c * P : (c + 1) * P],
+                        rhs=codes[:, o * N : o * N + count].bitcast(FP8X4),
+                        rhs_scale=scales[:, o * N : o * N + count],
+                        start=(o == 0),
+                        stop=(o == PASSES - 1),
+                    )
 
             last = T // P - 1
-            accs = [psum.tile([P, N], F32, name=("turned", "back")[c % 2]) for c in range(last)]
-            for o in range(PASSES):
-                for c in range(last):
-                    turned_pass(accs[c][:], o, c, N)
-            acc = psum.tile([P, P], F32, name="acc", bufs=4)
-            for o in range(PASSES):
-                turned_pass(acc[:], o, last, P)
-            ys_last = psum.tile([P, P], F32, name="acc", bufs=4)
-            for o in range(PASSES):
-                one_pass(ys_last[:], o, codes, scales, N, 1, words, planes, last * P, P)
-            return accs + [acc], ys_last
-
-        def keep_shared(accs):
-            start = landed[-1] - 4 * PASSES * PACK * P
-            for c, acc in enumerate(accs):
-                ys_turned.append(landing.tile([P, N], F32, name="ys_turned%d" % c, offset=start + 4 * N * c))
-                nc.scalar.copy(out=ys_turned[c][:, : acc.shape[1]], in_=acc[:])
+            for c0 in range(0, last, 2):
+                acc = psum.tile([P, 2, N], F32, name="turned")
+                for c in range(2):
+                    turned_product(acc[:, c, :], c0 + c, N)
+                nc.scalar.copy(out=ys_turned[:, c0 : c0 + 2, :], in_=acc[:])
+            acc = psum.tile([P, 2, P], F32, name="back")
+            turned_product(acc[:, 0, :], last, P)
+            product(acc[:, 1, :], codes, scales, N, 1, words, planes, last * P)
+            nc.scalar.copy(out=ys_turned[:, last, :P], in_=acc[:, 0, :])
+            nc.scalar.activation(out=ys_last[:], in_=acc[:, 1, :], func=IDENTITY, bias=bias[:, 1, SHARED : SHARED + 1])
 
         def spread_gate():
             turned = psum.tile([P, P], F32, name="turned")
             nc.tensor.transpose(turned[:], gate_rows[:], ident[:])
-            rows = TOP * T // P
-            nc.scalar.copy(out=gate_cols[:, :rows], in_=turned[:, :rows])
-            for first in range(0, rows, 4):
+            nc.scalar.copy(out=gate_cols[:], in_=turned[:])
+            for first in range(0, TOP * T // P, 4):
                 back = psum.tile([P, 4 * P], F32, name="back")
                 for i in range(4):
-                    column = gate_cols[:, first + i : first + i + 1].to_broadcast([P, P])
+                    r, c = divmod(first + i, T // P)
+                    column = gate_cols[:, 32 * r + c : 32 * r + c + 1].to_broadcast([P, P])
                     nc.tensor.transpose(back[:, i * P : (i + 1) * P], column, ident[:])
                 nc.scalar.copy(out=gate_sb[:, first * P : (first + 4) * P], in_=back[:])
 
+        def weigh_one(h, r, t0, count, dst):
+            nc.vector.tensor_tensor(
+                out=dst,
+                in0=y[h][:].indirect(pos_sb[r][:, t0 // 16 : (t0 + count) // 16]),
+                in1=gate_sb[:, r * T + t0 : r * T + t0 + count],
+                op=MULT,
+            )
+
         def weigh(h, t0, count):
-            products = keep.tile([P, TOP * count], F32, name="products%d_%d" % (h, t0))
-            for r in range(TOP):
-                nc.vector.tensor_tensor(
-                    out=products[:, r * count : (r + 1) * count],
-                    in0=y[h][:].indirect(pos_sb[r][:, t0 // 16 : (t0 + count) // 16]),
-                    in1=gate_sb[:, r * T + t0 : r * T + t0 + count],
-                    op=MULT,
-                )
+            products = ring.tile([P, TOP, count], F32, name="products")
+            for r in range(2):
+                weigh_one(h, r, t0, count, products[:, r, :])
+            for r in range(2, TOP):
+                window = y[h][:].indirect(pos_sb[r][:, t0 // 16 : (t0 + count) // 16])
+                nc.scalar.activation(out=products[:, r, :], in_=window, func=COPY)
+            weights = gate_sb[:].rearrange("p (r t) -> p r t", r=TOP)[:, 2:, t0 : t0 + count]
+            nc.vector.tensor_tensor(out=products[:, 2:, :], in0=products[:, 2:, :], in1=weights, op=MULT)
             return products
 
-        def add_turned(count, products):
-            totals = []
+        def add_turned(products, first, count, total):
+            turned = psum.tile([P, count], F32, name="turned")
             for c in range(0, count, P):
-                turned = psum.tile([P, P], F32, name="turned")
                 for r in range(TOP):
                     nc.tensor.matmul(
-                        turned[:], lhsT=products[:, r * count + c : r * count + c + P], rhs=ident[:],
+                        turned[:, c : c + P], lhsT=products[:, r, first + c : first + c + P], rhs=ident[:],
                         is_transpose=True, start=(r == 0), stop=(r == TOP - 1),
                     )
-                total = ring.tile([P, P], F32, name="total", bufs=2 * T // P)
-                nc.scalar.copy(out=total[:], in_=turned[:])
-                totals.append(total)
-            return totals
+            nc.scalar.copy(out=total, in_=turned[:])
 
-        def turn_back(h, t0, count, totals):
-            result = keep.tile([P, count], F32, name="result%d_%d" % (h, t0))
-            for c, total in enumerate(totals):
-                back = psum.tile([P, P], F32, name="back")
-                terms = (ys_turned[t0 // P + c][:, h * P : (h + 1) * P], total[:])
+        def turn_back(h, t0, count, total, result):
+            back = psum.tile([P, count], F32, name="back")
+            for c in range(0, count, P):
+                terms = (ys_turned[:, (t0 + c) // P, h * P : (h + 1) * P], total[:, c : c + P])
                 for i, term in enumerate(terms):
-                    nc.tensor.matmul(back[:], lhsT=term, rhs=ident[:], is_transpose=True, start=(i == 0), stop=(i == 1))
-                nc.scalar.activation(
-                    out=result[:, c * P : (c + 1) * P], in_=back[:], func=IDENTITY, bias=bias[:, h, SHARED : SHARED + 1]
-                )
-            nc.scalar.dma_start(out=out[h * P : (h + 1) * P, t0 : t0 + count], in_=result[:])
-
-        def finish_on_vector(h, t0, count, ys_last):
-            products = keep.tile([P, TOP * count], F32, name="products_last")
-            sums = ring.tile([P, TOP * count], F32, name="sums", bufs=1)
-            for r in range(TOP + 1):
-                if r < TOP:
-                    nc.vector.tensor_tensor(
-                        out=products[:, r * count : (r + 1) * count],
-                        in0=y[h][:].indirect(pos_sb[r][:, t0 // 16 : (t0 + count) // 16]),
-                        in1=gate_sb[:, r * T + t0 : r * T + t0 + count],
-                        op=MULT,
+                    nc.tensor.matmul(
+                        back[:, c : c + P], lhsT=term, rhs=ident[:], is_transpose=True, start=(i == 0), stop=(i == 1)
                     )
-                if r > 0:
-                    cols = slice((r - 1) * count, r * count)
-                    if r == 1:
-                        nc.vector.scalar_tensor_tensor(
-                            out=sums[:, cols], in0=ys_last[:], scalar=bias[:, h, SHARED : SHARED + 1],
-                            in1=products[:, cols], op0=ADD, op1=ADD,
-                        )
-                    else:
-                        before = sums[:, (r - 2) * count : (r - 1) * count]
-                        nc.vector.tensor_tensor(out=sums[:, cols], in0=before, in1=products[:, cols], op=ADD)
-            nc.sync.dma_start(out=out[h * P : (h + 1) * P, t0 : t0 + count], in_=sums[:, (TOP - 1) * count :])
+            nc.scalar.activation(out=result, in_=back[:], func=IDENTITY, bias=bias[:, h, SHARED : SHARED + 1])
 
-        both = tuple(range(HALVES))
+        def finish_on_vector(h, t0, count):
+            products = weigh(h, t0, count)
+            sums = keep.tile([P, TOP, count], F32, name="sums")
+            nc.vector.tensor_tensor(out=sums[:, 0, :], in0=products[:, 0, :], in1=ys_last[:], op=ADD)
+            nc.vector.tensor_tensor(out=sums[:, 1, :], in0=sums[:, 0, :], in1=products[:, 1, :], op=ADD)
+            nc.vector.tensor_tensor(out=sums[:, 2, :], in0=products[:, 2, :], in1=products[:, 3, :], op=ADD)
+            nc.vector.tensor_tensor(out=sums[:, 3, :], in0=sums[:, 1, :], in1=sums[:, 2, :], op=ADD)
+            nc.sync.dma_start(out=out[h * P : (h + 1) * P, t0 : t0 + count], in_=sums[:, TOP - 1, :])
+
+        nc.sync.dma_start(out=gate_rows[:], in_=gate.rearrange("r n (c t) -> r (n c) t", t=P)[:, :32, :])
+        nc.sync.dma_start(out=offs_sb[:], in_=offs)
+        for o in range(PASSES):
+            nc.sync.dma_start(out=words[o][:, :T], in_=x_words[o].rearrange("p t r -> p (t r)").bitcast(I32))
         for q in range(4):
             nc.scalar.dma_start(
                 out=planes[32 * q : 32 * q + 4 * PASSES, :T].bitcast(I32),
                 in_=x_scales[:, 4 * q : 4 * q + 4, :].bitcast(I32),
             )
-        nc.scalar.dma_start(out=gate_rows[: TOP * T // P, :], in_=gate[:, 0, :].rearrange("r (c t) -> r c t", t=P))
         nc.scalar.dma_start(out=bias[:, :, : E + 1], in_=b.rearrange("(h p) e -> p h e", p=P))
 
-        nc.sync.dma_start(out=offs_sb[:], in_=offs)
-        for o in range(PASSES):
-            nc.sync.dma_start(out=words[o][:, :T], in_=x_words[o].rearrange("p t r -> p (t r)").bitcast(I32))
-
-        def load(e):
+        def early(e):
             if e == 3:
                 for r, pos in enumerate((pos1, pos2, pos3, pos4)):
                     nc.sync.dma_start(out=pos_sb[r][:], in_=pos)
-            if e == 0 or e == E - 1:
-                return [load_pass(e, o, both) for o in range(PASSES)]
-            return load_whole(e)
+            return expert_by_pass(e, 0, N, 2) if e == 0 else whole_expert(e)
 
         spread_gate()
-        for experts in ((0, 1, 2, 3), (4, 5, 6, 7), (8, 9, 10, 11), (12, 13, 14, 15)):
-            add_bias(experts, both, routed_run(experts, both, load, 7))
-        for experts in ((16, 17, 18), (19,)):
-            accs = routed_run(experts, (0,), lambda e: [load_pass(e, o, (0,)) for o in range(PASSES)], 7)
-            add_bias(experts, (0,), accs)
-        shared_accs, ys_last = shared([load_pass(SHARED, o, both) for o in range(PASSES)])
-        first_products = weigh(0, 0, T)
-        for experts in ((16, 17, 18), (19,)):
-            accs = routed_run(experts, (1,), lambda e: [load_pass(e, o, (1,)) for o in range(PASSES)], 16)
-            add_bias(experts, (1,), accs)
-        keep_shared(shared_accs)
-        turn_back(0, 0, T, add_turned(T, first_products))
-        for t0, count in TOKEN_CHUNKS[:-1]:
-            turn_back(1, t0, count, add_turned(count, weigh(1, t0, count)))
-        finish_on_vector(1, *TOKEN_CHUNKS[-1], ys_last)
+        both = tuple(range(HALVES))
+        for e0 in range(0, 16, 4):
+            if e0 == SHARED_AFTER:
+                shared_expert()
+            routed_run(tuple(range(e0, e0 + 4)), both, early)
+        routed_run((16, 17, 18), both, early)
+        routed_run((19,), both, last_expert)
+
+        for h, t0, count in UNITS:
+            total = ring.tile([P, count], F32, name="total")
+            result = keep.tile([P, count], F32, name="result%d_%d" % (h, t0))
+            add_turned(weigh(h, t0, count), 0, count, total[:])
+            turn_back(h, t0, count, total[:], result[:])
+            nc.sync.dma_start(out=out[h * P : (h + 1) * P, t0 : t0 + count], in_=result[:])
+        finish_on_vector(1, 4 * P, P)

@@ -31,7 +31,8 @@ EXPERT_BYTES = 4 * PASSES * PACK * N
 LANDING_BYTES = 7 * EXPERT_BYTES
 WHOLE_SCALAR_COLS = 200
 SHARED_AFTER = 8
-UNITS = ((0, 0, 256), (0, 256, 256), (0, 512, 128), (1, 0, 256), (1, 256, 128), (1, 384, 128))
+BANK_BYTES = 2048
+PIECES = ((0, 3 * P), (3 * P, 2 * P))
 
 
 def tile_moe_shr_lin_bias_kernel(
@@ -42,7 +43,7 @@ def tile_moe_shr_lin_bias_kernel(
         keep = ctx.enter_context(tc.tile_pool(name="keep", bufs=1))
         ring = ctx.enter_context(tc.tile_pool(name="ring", bufs=2))
         landing = ctx.enter_context(tc.tile_pool(name="landing", bufs=1))
-        psum = ctx.enter_context(tc.psum_pool(name="psum", bufs=2))
+        psum = ctx.enter_context(tc.psum_pool(name="psum", bufs=1))
 
         offs_sb = keep.tile([P, SLOTS // 16], U16, name="offs_sb")
         pos_sb = [keep.tile([P, T // 16], U16, name="pos_sb%d" % r) for r in range(TOP)]
@@ -51,16 +52,21 @@ def tile_moe_shr_lin_bias_kernel(
         bias = keep.tile([P, HALVES, 24], F32, name="bias")
         gate_rows = keep.tile([P, P], F32, name="gate_rows")
         gate_cols = keep.tile([P, P], F32, name="gate_cols")
-        gate_sb = keep.tile([P, TOP * T], F32, name="gate_sb")
+        gate_sb = keep.tile([P, T], F32, name="gate_sb")
         ident = keep.tile([P, P], F32, name="ident")
         y = [keep.tile([P, SLOTS], F32, name="y%d" % h) for h in range(HALVES)]
         ys_turned = keep.tile([P, T // P, N], F32, name="ys_turned")
-        ys_last = keep.tile([P, P], F32, name="ys_last")
 
         nc.vector.memset(planes[:].bitcast(I32), 0)
         for o in range(PASSES):
             nc.vector.memset(words[o][:, T:], 0)
         make_identity(nc, ident[:])
+
+        banks_taken = []
+
+        def bank(number, shape):
+            banks_taken.append(number)
+            return psum.tile(shape, F32, name="bank%d" % len(banks_taken), offset=number * BANK_BYTES)
 
         landed = [0]
 
@@ -165,9 +171,9 @@ def tile_moe_shr_lin_bias_kernel(
                 gathered.setdefault(g, gather_tokens(g))
             return gathered[g] + (first,)
 
-        def routed_run(experts, halves, prepare):
+        def routed_run(experts, halves, prepare, first_bank):
             width = len(halves) * P
-            accs = [psum.tile([P, len(experts) * C], F32, name="acc", bufs=4) for h in halves]
+            accs = [bank(first_bank + h, [P, len(experts) * C]) for h in halves]
             for n, e in enumerate(experts):
                 codes, scales = prepare(e)
                 slots = slots_of(e)
@@ -208,77 +214,53 @@ def tile_moe_shr_lin_bias_kernel(
                         stop=(o == PASSES - 1),
                     )
 
-            last = T // P - 1
-            for c0 in range(0, last, 2):
-                acc = psum.tile([P, 2, N], F32, name="turned")
-                for c in range(2):
+            for c0 in range(0, T // P, 2):
+                count = min(2, T // P - c0)
+                acc = bank(4 + c0 // 2, [P, count, N])
+                for c in range(count):
                     turned_product(acc[:, c, :], c0 + c, N)
-                nc.scalar.copy(out=ys_turned[:, c0 : c0 + 2, :], in_=acc[:])
-            acc = psum.tile([P, 2, P], F32, name="back")
-            turned_product(acc[:, 0, :], last, P)
-            product(acc[:, 1, :], codes, scales, N, 1, words, planes, last * P)
-            nc.scalar.copy(out=ys_turned[:, last, :P], in_=acc[:, 0, :])
-            nc.scalar.activation(out=ys_last[:], in_=acc[:, 1, :], func=IDENTITY, bias=bias[:, 1, SHARED : SHARED + 1])
+                nc.scalar.copy(out=ys_turned[:, c0 : c0 + count, :], in_=acc[:])
 
         def spread_gate():
-            turned = psum.tile([P, P], F32, name="turned")
+            turned = bank(4, [P, P])
             nc.tensor.transpose(turned[:], gate_rows[:], ident[:])
             nc.scalar.copy(out=gate_cols[:], in_=turned[:])
-            for first in range(0, TOP * T // P, 4):
-                back = psum.tile([P, 4 * P], F32, name="back")
-                for i in range(4):
-                    r, c = divmod(first + i, T // P)
-                    column = gate_cols[:, 32 * r + c : 32 * r + c + 1].to_broadcast([P, P])
-                    nc.tensor.transpose(back[:, i * P : (i + 1) * P], column, ident[:])
-                nc.scalar.copy(out=gate_sb[:, first * P : (first + 4) * P], in_=back[:])
+            for i, (t0, count) in enumerate(PIECES):
+                back = bank(5 + i, [P, count])
+                for c in range(0, count, P):
+                    col = 32 * (TOP - 1) + (t0 + c) // P
+                    column = gate_cols[:, col : col + 1].to_broadcast([P, P])
+                    nc.tensor.transpose(back[:, c : c + P], column, ident[:])
+                nc.scalar.copy(out=gate_sb[:, t0 : t0 + count], in_=back[:])
 
-        def weigh_one(h, r, t0, count, dst):
-            nc.vector.tensor_tensor(
-                out=dst,
-                in0=y[h][:].indirect(pos_sb[r][:, t0 // 16 : (t0 + count) // 16]),
-                in1=gate_sb[:, r * T + t0 : r * T + t0 + count],
-                op=MULT,
-            )
-
-        def weigh(h, t0, count):
-            products = ring.tile([P, TOP, count], F32, name="products")
-            for r in range(2):
-                weigh_one(h, r, t0, count, products[:, r, :])
-            for r in range(2, TOP):
-                window = y[h][:].indirect(pos_sb[r][:, t0 // 16 : (t0 + count) // 16])
-                nc.scalar.activation(out=products[:, r, :], in_=window, func=COPY)
-            weights = gate_sb[:].rearrange("p (r t) -> p r t", r=TOP)[:, 2:, t0 : t0 + count]
-            nc.vector.tensor_tensor(out=products[:, 2:, :], in0=products[:, 2:, :], in1=weights, op=MULT)
-            return products
-
-        def add_turned(products, first, count, total):
-            turned = psum.tile([P, count], F32, name="turned")
-            for c in range(0, count, P):
-                for r in range(TOP):
+        def add_back(sums, term, first, last):
+            for acc, (t0, count) in zip(sums, PIECES):
+                for c in range(0, count, P):
                     nc.tensor.matmul(
-                        turned[:, c : c + P], lhsT=products[:, r, first + c : first + c + P], rhs=ident[:],
-                        is_transpose=True, start=(r == 0), stop=(r == TOP - 1),
+                        acc[:, c : c + P], lhsT=term((t0 + c) // P), rhs=ident[:], is_transpose=True,
+                        start=(first and c == 0), stop=(last and c == count - P),
                     )
-            nc.scalar.copy(out=total, in_=turned[:])
 
-        def turn_back(h, t0, count, total, result):
-            back = psum.tile([P, count], F32, name="back")
-            for c in range(0, count, P):
-                terms = (ys_turned[:, (t0 + c) // P, h * P : (h + 1) * P], total[:, c : c + P])
-                for i, term in enumerate(terms):
-                    nc.tensor.matmul(
-                        back[:, c : c + P], lhsT=term, rhs=ident[:], is_transpose=True, start=(i == 0), stop=(i == 1)
+        def open_sums(h):
+            sums = [bank(4 + 2 * h + i, [P, count]) for i, (t0, count) in enumerate(PIECES)]
+            add_back(sums, lambda c: ys_turned[:, c, h * P : (h + 1) * P], True, False)
+            return sums
+
+        def weigh_turned(h, r, sums, last):
+            fetched = ring.tile([P, T], F32, name="fetched", bufs=3)
+            weighed = ring.tile([P, T], F32, name="weighed", bufs=3)
+            nc.vector.tensor_copy(out=fetched[:], in_=y[h][:].indirect(pos_sb[r][:]))
+            for i, (t0, count) in enumerate(PIECES):
+                turned = bank(2 * (r % 2) + i, [P, count])
+                for c in range(0, count, P):
+                    nc.tensor.transpose(turned[:, c : c + P], fetched[:, t0 + c : t0 + c + P], ident[:])
+                for c in range(0, count, P):
+                    col = 32 * r + (t0 + c) // P
+                    nc.scalar.activation(
+                        out=weighed[:, t0 + c : t0 + c + P], in_=turned[:, c : c + P], func=COPY,
+                        scale=gate_cols[:, col : col + 1],
                     )
-            nc.scalar.activation(out=result, in_=back[:], func=IDENTITY, bias=bias[:, h, SHARED : SHARED + 1])
-
-        def finish_on_vector(h, t0, count):
-            products = weigh(h, t0, count)
-            sums = keep.tile([P, TOP, count], F32, name="sums")
-            nc.vector.tensor_tensor(out=sums[:, 0, :], in0=products[:, 0, :], in1=ys_last[:], op=ADD)
-            nc.vector.tensor_tensor(out=sums[:, 1, :], in0=sums[:, 0, :], in1=products[:, 1, :], op=ADD)
-            nc.vector.tensor_tensor(out=sums[:, 2, :], in0=products[:, 2, :], in1=products[:, 3, :], op=ADD)
-            nc.vector.tensor_tensor(out=sums[:, 3, :], in0=sums[:, 1, :], in1=sums[:, 2, :], op=ADD)
-            nc.sync.dma_start(out=out[h * P : (h + 1) * P, t0 : t0 + count], in_=sums[:, TOP - 1, :])
+            add_back(sums, lambda c: weighed[:, c * P : (c + 1) * P], False, last)
 
         nc.sync.dma_start(out=gate_rows[:], in_=gate.rearrange("r n (c t) -> r (n c) t", t=P)[:, :32, :])
         nc.sync.dma_start(out=offs_sb[:], in_=offs)
@@ -302,14 +284,32 @@ def tile_moe_shr_lin_bias_kernel(
         for e0 in range(0, 16, 4):
             if e0 == SHARED_AFTER:
                 shared_expert()
-            routed_run(tuple(range(e0, e0 + 4)), both, early)
-        routed_run((16, 17, 18), both, early)
-        routed_run((19,), both, last_expert)
+            routed_run(tuple(range(e0, e0 + 4)), both, early, e0 // 2 % 4)
+        sums = [open_sums(h) for h in both]
+        routed_run((16, 17, 18), both, early, 0)
+        routed_run((19,), both, last_expert, 2)
 
-        for h, t0, count in UNITS:
-            total = ring.tile([P, count], F32, name="total")
-            result = keep.tile([P, count], F32, name="result%d_%d" % (h, t0))
-            add_turned(weigh(h, t0, count), 0, count, total[:])
-            turn_back(h, t0, count, total[:], result[:])
-            nc.sync.dma_start(out=out[h * P : (h + 1) * P, t0 : t0 + count], in_=result[:])
-        finish_on_vector(1, 4 * P, P)
+        results = [keep.tile([P, T], F32, name="result%d" % h) for h in both]
+        for r in range(TOP):
+            weigh_turned(0, r, sums[0], r == TOP - 1)
+        for acc, (t0, count) in zip(sums[0], PIECES):
+            nc.scalar.activation(
+                out=results[0][:, t0 : t0 + count], in_=acc[:], func=IDENTITY, bias=bias[:, 0, SHARED : SHARED + 1]
+            )
+        nc.sync.dma_start(out=out[:P, :], in_=results[0][:])
+        for r in range(TOP - 1):
+            weigh_turned(1, r, sums[1], r == TOP - 2)
+        products = keep.tile([P, T], F32, name="products")
+        for t0, count in PIECES:
+            nc.vector.tensor_tensor(
+                out=products[:, t0 : t0 + count],
+                in0=y[1][:].indirect(pos_sb[TOP - 1][:, t0 // 16 : (t0 + count) // 16]),
+                in1=gate_sb[:, t0 : t0 + count],
+                op=MULT,
+            )
+        for acc, (t0, count) in zip(sums[1], PIECES):
+            nc.vector.scalar_tensor_tensor(
+                out=results[1][:, t0 : t0 + count], in0=acc[:], scalar=bias[:, 1, SHARED : SHARED + 1],
+                in1=products[:, t0 : t0 + count], op0=ADD, op1=ADD,
+            )
+            nc.sync.dma_start(out=out[P:, t0 : t0 + count], in_=results[1][:, t0 : t0 + count])

@@ -30,9 +30,11 @@ WINDOW = 704
 EXPERT_BYTES = 4 * PASSES * PACK * N
 LANDING_BYTES = 7 * EXPERT_BYTES
 WHOLE_SCALAR_COLS = 200
-SHARED_AFTER = 8
 BANK_BYTES = 2048
-PIECES = ((0, 3 * P), (3 * P, 2 * P))
+BY_PASS = 17
+LATE_VECTOR_COLS = 96
+THROUGH = 3 * P
+PIECES = (((0, 4 * P), (4 * P, P)), ((0, THROUGH),))
 
 
 def tile_moe_shr_lin_bias_kernel(
@@ -52,7 +54,7 @@ def tile_moe_shr_lin_bias_kernel(
         bias = keep.tile([P, HALVES, 24], F32, name="bias")
         gate_rows = keep.tile([P, P], F32, name="gate_rows")
         gate_cols = keep.tile([P, P], F32, name="gate_cols")
-        gate_sb = keep.tile([P, T], F32, name="gate_sb")
+        gate_sb = keep.tile([P, TOP, T], F32, name="gate_sb")
         ident = keep.tile([P, P], F32, name="ident")
         y = [keep.tile([P, SLOTS], F32, name="y%d" % h) for h in range(HALVES)]
         ys_turned = keep.tile([P, T // P, N], F32, name="ys_turned")
@@ -123,26 +125,26 @@ def tile_moe_shr_lin_bias_kernel(
                     nc.vector.tensor_copy(out=dst, in_=src)
             return quantize(codes, scales, stage, width)
 
-        def last_expert(e):
+        def late_expert(e):
             raws = [load_pass(e, o, 0, N) for o in range(PASSES)]
             codes, scales, stage = mx_tiles(N)
-            pieces = [(o * N, N, raws[o]) for o in range(PASSES - 1)]
-            pieces.extend([(2 * N + h * P, P, raws[2][:, :, h * P : (h + 1) * P]) for h in range(HALVES)])
-            for n, (first, width, raw) in enumerate(pieces):
-                flat = stage[:, PACK * first : PACK * (first + width)]
-                dst = flat.rearrange("p (c i j) -> p c j i", i=4, j=PACK)
-                src = raw.rearrange("p j (c i) -> p c j i", i=4)
-                if n == 2:
-                    nc.vector.tensor_copy(out=dst, in_=src)
-                else:
-                    nc.scalar.copy(out=dst, in_=src)
-                cols = slice(first, first + width)
-                nc.vector.quantize_mx(out=codes[:, cols].bitcast(FP8X4), scales=scales[:, cols], in_=flat)
+            for o in range(PASSES):
+                final = (e, o) == (E - 1, PASSES - 1)
+                cut = (P if final else LATE_VECTOR_COLS) // 4
+                dst = stage[:, PACK * o * N : PACK * (o + 1) * N].rearrange("p (c i j) -> p c j i", i=4, j=PACK)
+                src = raws[o].rearrange("p j (c i) -> p c j i", i=4)
+                nc.vector.tensor_copy(out=dst[:, :cut], in_=src[:, :cut])
+                nc.scalar.copy(out=dst[:, cut:], in_=src[:, cut:])
+                width = P if final else N
+                for first in range(o * N, (o + 1) * N, width):
+                    cols = slice(first, first + width)
+                    flat = stage[:, PACK * first : PACK * (first + width)]
+                    nc.vector.quantize_mx(out=codes[:, cols].bitcast(FP8X4), scales=scales[:, cols], in_=flat)
             return codes, scales
 
         def gather_tokens(g):
-            slot_words = ring.tile([P, PASSES * GATHER], U32, name="slot_words", align_bytes=64)
-            slot_planes = ring.tile([P, GATHER], U8, name="slot_planes", align_bytes=64)
+            slot_words = ring.tile([P, PASSES * GATHER], U32, name="slot_words", bufs=3, align_bytes=64)
+            slot_planes = ring.tile([P, GATHER], U8, name="slot_planes", bufs=3, align_bytes=64)
             entries = offs_sb[:, g * GATHER // 16 : (g + 1) * GATHER // 16]
             for o in range(PASSES):
                 window = words[o][:].bitcast(U32)
@@ -150,15 +152,15 @@ def tile_moe_shr_lin_bias_kernel(
             nc.vector.tensor_copy(out=slot_planes[:], in_=planes[:].indirect(entries))
             return [slot_words[:, o * GATHER : (o + 1) * GATHER] for o in range(PASSES)], slot_planes
 
-        def product(acc, codes, scales, width, i, moving, moving_planes, first, passes=range(PASSES)):
+        def product(acc, codes, scales, width, i, moving, moving_planes, first, count=P, passes=range(PASSES)):
             for o in passes:
                 cols = slice(o * width + i * P, o * width + (i + 1) * P)
                 nc.tensor.matmul_mx(
                     out=acc,
                     lhsT=codes[:, cols].bitcast(FP8X4),
                     lhsT_scale=scales[:, cols],
-                    rhs=moving[o][:, first : first + P].bitcast(FP8X4),
-                    rhs_scale=moving_planes[4 * o :, first : first + P],
+                    rhs=moving[o][:, first : first + count].bitcast(FP8X4),
+                    rhs_scale=moving_planes[4 * o :, first : first + count],
                     start=(o == 0),
                     stop=(o == PASSES - 1),
                 )
@@ -187,7 +189,7 @@ def tile_moe_shr_lin_bias_kernel(
             e0, count = experts[0], len(experts)
             for acc, h in zip(accs, halves):
                 dst = y[h][:, e0 * C : (e0 + count) * C]
-                if count == 1 and h == 1:
+                if e0 == E - 1 and h == 1:
                     nc.scalar.activation(out=dst, in_=acc[:], func=IDENTITY, bias=bias[:, h, e0 : e0 + 1])
                 elif count == 1:
                     nc.vector.tensor_scalar(out=dst, in0=acc[:], scalar1=bias[:, h, e0 : e0 + 1], scalar2=None, op0=ADD)
@@ -200,69 +202,108 @@ def tile_moe_shr_lin_bias_kernel(
                     )
 
         def shared_expert():
-            codes, scales = whole_expert(SHARED)
-
-            def turned_product(acc, c, count):
-                for o in range(PASSES):
-                    nc.tensor.matmul_mx(
-                        out=acc,
-                        lhsT=words[o][:, c * P : (c + 1) * P].bitcast(FP8X4),
-                        lhsT_scale=planes[4 * o :, c * P : (c + 1) * P],
-                        rhs=codes[:, o * N : o * N + count].bitcast(FP8X4),
-                        rhs_scale=scales[:, o * N : o * N + count],
-                        start=(o == 0),
-                        stop=(o == PASSES - 1),
-                    )
-
-            for c0 in range(0, T // P, 2):
-                count = min(2, T // P - c0)
-                acc = bank(4 + c0 // 2, [P, count, N])
-                for c in range(count):
-                    turned_product(acc[:, c, :], c0 + c, N)
-                nc.scalar.copy(out=ys_turned[:, c0 : c0 + count, :], in_=acc[:])
+            raws = [load_pass(SHARED, o, 0, N) for o in range(PASSES)]
+            codes, scales, stage = mx_tiles(N)
+            layout = ((4, (0, 1), N), (5, (2,), N), (6, (3, 4), P))
+            accs = [bank(number, [P, len(chunks), width]) for number, chunks, width in layout]
+            rows = bank(7, [P, T - THROUGH])
+            for o in range(PASSES):
+                flat = stage[:, o * PACK * N : (o + 1) * PACK * N]
+                dst = flat.rearrange("p (c i j) -> p c j i", i=4, j=PACK)
+                src = raws[o].rearrange("p j (c i) -> p c j i", i=4)
+                if o < PASSES - 1:
+                    nc.scalar.copy(out=dst, in_=src)
+                else:
+                    nc.vector.tensor_copy(out=dst, in_=src)
+                cols = slice(o * N, (o + 1) * N)
+                nc.vector.quantize_mx(out=codes[:, cols].bitcast(FP8X4), scales=scales[:, cols], in_=flat)
+                for acc, (number, chunks, width) in zip(accs, layout):
+                    for i, c in enumerate(chunks):
+                        nc.tensor.matmul_mx(
+                            out=acc[:, i, :],
+                            lhsT=words[o][:, c * P : (c + 1) * P].bitcast(FP8X4),
+                            lhsT_scale=planes[4 * o :, c * P : (c + 1) * P],
+                            rhs=codes[:, o * N : o * N + width].bitcast(FP8X4),
+                            rhs_scale=scales[:, o * N : o * N + width],
+                            start=(o == 0 and i == 0),
+                            stop=(o == PASSES - 1 and i == len(chunks) - 1),
+                        )
+                product(rows[:], codes, scales, N, 1, words, planes, THROUGH, T - THROUGH, (o,))
+            for acc, (number, chunks, width) in zip(accs, layout):
+                nc.scalar.copy(out=ys_turned[:, chunks[0] : chunks[-1] + 1, :width], in_=acc[:])
+            return rows
 
         def spread_gate():
             turned = bank(4, [P, P])
             nc.tensor.transpose(turned[:], gate_rows[:], ident[:])
             nc.scalar.copy(out=gate_cols[:], in_=turned[:])
-            for i, (t0, count) in enumerate(PIECES):
-                back = bank(5 + i, [P, count])
-                for c in range(0, count, P):
-                    col = 32 * (TOP - 1) + (t0 + c) // P
-                    column = gate_cols[:, col : col + 1].to_broadcast([P, P])
-                    nc.tensor.transpose(back[:, c : c + P], column, ident[:])
-                nc.scalar.copy(out=gate_sb[:, t0 : t0 + count], in_=back[:])
+            flat = gate_sb[:].rearrange("p r t -> p (r t)")
+            for first in range(0, TOP * T // P, 4):
+                back = bank(5 + first // 4 % 3, [P, 4 * P])
+                for i in range(4):
+                    r, c = divmod(first + i, T // P)
+                    column = gate_cols[:, TOP * c + r : TOP * c + r + 1].to_broadcast([P, P])
+                    nc.tensor.transpose(back[:, i * P : (i + 1) * P], column, ident[:])
+                nc.scalar.copy(out=flat[:, first * P : (first + 4) * P], in_=back[:])
 
-        def add_back(sums, term, first, last):
-            for acc, (t0, count) in zip(sums, PIECES):
+        def add_back(h, sums, term, first):
+            for acc, (t0, count) in zip(sums, PIECES[h]):
                 for c in range(0, count, P):
                     nc.tensor.matmul(
                         acc[:, c : c + P], lhsT=term((t0 + c) // P), rhs=ident[:], is_transpose=True,
-                        start=(first and c == 0), stop=(last and c == count - P),
+                        start=(first and c == 0), stop=(not first and c == count - P),
                     )
 
         def open_sums(h):
-            sums = [bank(4 + 2 * h + i, [P, count]) for i, (t0, count) in enumerate(PIECES)]
-            add_back(sums, lambda c: ys_turned[:, c, h * P : (h + 1) * P], True, False)
+            sums = [bank(4 + 2 * h + i, [P, count]) for i, (t0, count) in enumerate(PIECES[h])]
+            add_back(h, sums, lambda c: ys_turned[:, c, h * P : (h + 1) * P], True)
             return sums
 
-        def weigh_turned(h, r, sums, last):
-            fetched = ring.tile([P, T], F32, name="fetched", bufs=3)
-            weighed = ring.tile([P, T], F32, name="weighed", bufs=3)
-            nc.vector.tensor_copy(out=fetched[:], in_=y[h][:].indirect(pos_sb[r][:]))
-            for i, (t0, count) in enumerate(PIECES):
-                turned = bank(2 * (r % 2) + i, [P, count])
-                for c in range(0, count, P):
-                    nc.tensor.transpose(turned[:, c : c + P], fetched[:, t0 + c : t0 + c + P], ident[:])
-                for c in range(0, count, P):
-                    col = 32 * r + (t0 + c) // P
-                    nc.scalar.activation(
-                        out=weighed[:, t0 + c : t0 + c + P], in_=turned[:, c : c + P], func=COPY,
-                        scale=gate_cols[:, col : col + 1],
-                    )
-            add_back(sums, lambda c: weighed[:, c * P : (c + 1) * P], False, last)
+        def fetched(h, r, t0, count):
+            return y[h][:].indirect(pos_sb[r][:, t0 // 16 : (t0 + count) // 16])
 
-        nc.sync.dma_start(out=gate_rows[:], in_=gate.rearrange("r n (c t) -> r (n c) t", t=P)[:, :32, :])
+        def fetch_plain(h, lists, t0, count, tag):
+            plain = keep.tile([P, len(lists), count], F32, name="plain%d_%d" % (h, t0), tag=tag)
+            for i, r in enumerate(lists):
+                nc.scalar.activation(out=plain[:, i, :], in_=fetched(h, r, t0, count), func=COPY)
+            return plain
+
+        def fetch_weighed(h, lists, t0, count, tag):
+            products = keep.tile([P, len(lists), count], F32, name="fetched%d_%d" % (h, lists[0]), tag=tag)
+            for i, r in enumerate(lists):
+                nc.vector.tensor_tensor(
+                    out=products[:, i, :], in0=fetched(h, r, t0, count), in1=gate_sb[:, r, t0 : t0 + count], op=MULT
+                )
+            return [products[:, i, :] for i in range(len(lists))]
+
+        def weigh(h, plain, lists, t0, count):
+            products = keep.tile([P, len(lists), count], F32, name="weighed%d_%d" % (h, t0))
+            weights = gate_sb[:, lists[0] : lists[-1] + 1, t0 : t0 + count]
+            nc.vector.tensor_tensor(out=products[:], in0=plain[:], in1=weights, op=MULT)
+            return [products[:, i, :] for i in range(len(lists))]
+
+        def add_up(h, products):
+            total = keep.tile([P, products[0].shape[1]], F32, name="total%d" % h)
+            result = keep.tile([P, products[0].shape[1]], F32, name="result%d" % h)
+            turned = [bank(2 * h + i, [P, count]) for i, (t0, count) in enumerate(PIECES[h])]
+            for r in range(TOP):
+                for acc, (t0, count) in zip(turned, PIECES[h]):
+                    for c in range(0, count, P):
+                        nc.tensor.matmul(
+                            acc[:, c : c + P], lhsT=products[r][:, t0 + c : t0 + c + P], rhs=ident[:],
+                            is_transpose=True, start=(r == 0 and c == 0), stop=(r == TOP - 1 and c == count - P),
+                        )
+            for acc, (t0, count) in zip(turned, PIECES[h]):
+                nc.scalar.copy(out=total[:, t0 : t0 + count], in_=acc[:])
+            sums = open_sums(h)
+            add_back(h, sums, lambda c: total[:, c * P : (c + 1) * P], False)
+            for acc, (t0, count) in zip(sums, PIECES[h]):
+                nc.scalar.activation(
+                    out=result[:, t0 : t0 + count], in_=acc[:], func=IDENTITY, bias=bias[:, h, SHARED : SHARED + 1]
+                )
+            nc.scalar.dma_start(out=out[h * P : (h + 1) * P, : products[0].shape[1]], in_=result[:])
+
+        nc.sync.dma_start(out=gate_rows[:], in_=gate.rearrange("r n (c t) -> (n c) r t", t=P)[:32])
         nc.sync.dma_start(out=offs_sb[:], in_=offs)
         for o in range(PASSES):
             nc.sync.dma_start(out=words[o][:, :T], in_=x_words[o].rearrange("p t r -> p (t r)").bitcast(I32))
@@ -277,39 +318,42 @@ def tile_moe_shr_lin_bias_kernel(
             if e == 3:
                 for r, pos in enumerate((pos1, pos2, pos3, pos4)):
                     nc.sync.dma_start(out=pos_sb[r][:], in_=pos)
-            return expert_by_pass(e, 0, N, 2) if e == 0 else whole_expert(e)
+            if e >= BY_PASS:
+                return late_expert(e)
+            return expert_by_pass(e, 0, N, 3) if e == 0 else whole_expert(e)
 
         spread_gate()
         both = tuple(range(HALVES))
         for e0 in range(0, 16, 4):
-            if e0 == SHARED_AFTER:
-                shared_expert()
             routed_run(tuple(range(e0, e0 + 4)), both, early, e0 // 2 % 4)
-        sums = [open_sums(h) for h in both]
-        routed_run((16, 17, 18), both, early, 0)
-        routed_run((19,), both, last_expert, 2)
+        routed_run((16, 17), both, early, 0)
+        routed_run((18,), both, early, 2)
+        routed_run((19,), both, early, 0)
+        shared_rows = shared_expert()
 
-        results = [keep.tile([P, T], F32, name="result%d" % h) for h in both]
+        rest = T - THROUGH
+        plain = fetch_plain(0, (2, 3), 0, T, "first_plain")
+        first = fetch_weighed(0, (0, 1), 0, T, "first_fetched") + weigh(0, plain, (2, 3), 0, T)
+        plain = fetch_plain(1, (3,), 0, THROUGH, "second_plain")
+        second = fetch_weighed(1, (0,), 0, THROUGH, "second_fetched")
+        second = second + fetch_weighed(1, (1, 2), 0, THROUGH, "first_plain") + weigh(1, plain, (3,), 0, THROUGH)
+        add_up(0, first)
+        add_up(1, second)
+
+        plain = fetch_plain(1, (3,), THROUGH, rest, "last_plain")
+        last = weigh(1, plain, (3,), THROUGH, rest)
+        products = keep.tile([P, TOP - 1, rest], F32, name="last_fetched", tag="second_plain")
+        steps = keep.tile([P, TOP, rest], F32, name="steps")
         for r in range(TOP):
-            weigh_turned(0, r, sums[0], r == TOP - 1)
-        for acc, (t0, count) in zip(sums[0], PIECES):
-            nc.scalar.activation(
-                out=results[0][:, t0 : t0 + count], in_=acc[:], func=IDENTITY, bias=bias[:, 0, SHARED : SHARED + 1]
-            )
-        nc.sync.dma_start(out=out[:P, :], in_=results[0][:])
-        for r in range(TOP - 1):
-            weigh_turned(1, r, sums[1], r == TOP - 2)
-        products = keep.tile([P, T], F32, name="products")
-        for t0, count in PIECES:
-            nc.vector.tensor_tensor(
-                out=products[:, t0 : t0 + count],
-                in0=y[1][:].indirect(pos_sb[TOP - 1][:, t0 // 16 : (t0 + count) // 16]),
-                in1=gate_sb[:, t0 : t0 + count],
-                op=MULT,
-            )
-        for acc, (t0, count) in zip(sums[1], PIECES):
-            nc.vector.scalar_tensor_tensor(
-                out=results[1][:, t0 : t0 + count], in0=acc[:], scalar=bias[:, 1, SHARED : SHARED + 1],
-                in1=products[:, t0 : t0 + count], op0=ADD, op1=ADD,
-            )
-            nc.sync.dma_start(out=out[P:, t0 : t0 + count], in_=results[1][:, t0 : t0 + count])
+            if r < TOP - 1:
+                nc.vector.tensor_tensor(
+                    out=products[:, r, :], in0=fetched(1, r, THROUGH, rest), in1=gate_sb[:, r, THROUGH:], op=MULT
+                )
+            if r == 0:
+                nc.vector.scalar_tensor_tensor(
+                    out=steps[:, 0, :], in0=shared_rows[:], scalar=bias[:, 1, SHARED : SHARED + 1],
+                    in1=last[0], op0=ADD, op1=ADD,
+                )
+            else:
+                nc.vector.tensor_tensor(out=steps[:, r, :], in0=steps[:, r - 1, :], in1=products[:, r - 1, :], op=ADD)
+        nc.sync.dma_start(out=out[P:, THROUGH:], in_=steps[:, 3, :])

@@ -53,7 +53,7 @@ def tile_moe_shr_lin_bias_kernel(
         planes = keep.tile([P, WINDOW], U8, name="planes", align_bytes=64)
         bias = keep.tile([P, HALVES, 24], F32, name="bias")
         gate_rows = keep.tile([P, P], F32, name="gate_rows")
-        gate_cols = keep.tile([P, P], F32, name="gate_cols")
+        gate_cols = keep.tile([P, TOP * T // P], F32, name="gate_cols")
         gate_sb = keep.tile([P, TOP, T], F32, name="gate_sb")
         ident = keep.tile([P, P], F32, name="ident")
         y = [keep.tile([P, SLOTS], F32, name="y%d" % h) for h in range(HALVES)]
@@ -62,6 +62,7 @@ def tile_moe_shr_lin_bias_kernel(
         nc.vector.memset(planes[:].bitcast(I32), 0)
         for o in range(PASSES):
             nc.vector.memset(words[o][:, T:], 0)
+        nc.gpsimd.memset(gate_rows[:], 0.0)
         make_identity(nc, ident[:])
 
         banks_taken = []
@@ -111,19 +112,6 @@ def tile_moe_shr_lin_bias_kernel(
             nc.scalar.copy(out=dst[:, :cut], in_=src[:, :cut])
             nc.vector.tensor_copy(out=dst[:, cut:], in_=src[:, cut:])
             return quantize(codes, scales, stage, N)
-
-        def expert_by_pass(e, first, width, scalar_passes):
-            raws = [load_pass(e, o, first, width) for o in range(PASSES)]
-            codes, scales, stage = mx_tiles(width)
-            for o in range(PASSES):
-                dst = stage[:, o * PACK * width : (o + 1) * PACK * width]
-                dst = dst.rearrange("p (c i j) -> p c j i", i=4, j=PACK)
-                src = raws[o].rearrange("p j (c i) -> p c j i", i=4)
-                if o < scalar_passes:
-                    nc.scalar.copy(out=dst, in_=src)
-                else:
-                    nc.vector.tensor_copy(out=dst, in_=src)
-            return quantize(codes, scales, stage, width)
 
         def late_expert(e):
             raws = [load_pass(e, o, 0, N) for o in range(PASSES)]
@@ -236,7 +224,7 @@ def tile_moe_shr_lin_bias_kernel(
         def spread_gate():
             turned = bank(4, [P, P])
             nc.tensor.transpose(turned[:], gate_rows[:], ident[:])
-            nc.scalar.copy(out=gate_cols[:], in_=turned[:])
+            nc.scalar.copy(out=gate_cols[:], in_=turned[:, : TOP * T // P])
             flat = gate_sb[:].rearrange("p r t -> p (r t)")
             for first in range(0, TOP * T // P, 4):
                 back = bank(5 + first // 4 % 3, [P, 4 * P])
@@ -303,7 +291,6 @@ def tile_moe_shr_lin_bias_kernel(
                 )
             nc.scalar.dma_start(out=out[h * P : (h + 1) * P, : products[0].shape[1]], in_=result[:])
 
-        nc.sync.dma_start(out=gate_rows[:], in_=gate.rearrange("r n (c t) -> (n c) r t", t=P)[:32])
         nc.sync.dma_start(out=offs_sb[:], in_=offs)
         for o in range(PASSES):
             nc.sync.dma_start(out=words[o][:, :T], in_=x_words[o].rearrange("p t r -> p (t r)").bitcast(I32))
@@ -312,17 +299,22 @@ def tile_moe_shr_lin_bias_kernel(
                 out=planes[32 * q : 32 * q + 4 * PASSES, :T].bitcast(I32),
                 in_=x_scales[:, 4 * q : 4 * q + 4, :].bitcast(I32),
             )
-        nc.scalar.dma_start(out=bias[:, :, : E + 1], in_=b.rearrange("(h p) e -> p h e", p=P))
 
         def early(e):
-            if e == 3:
-                for r, pos in enumerate((pos1, pos2, pos3, pos4)):
-                    nc.sync.dma_start(out=pos_sb[r][:], in_=pos)
             if e >= BY_PASS:
                 return late_expert(e)
-            return expert_by_pass(e, 0, N, 3) if e == 0 else whole_expert(e)
+            prepared = whole_expert(e)
+            if e == 2:
+                nc.sync.dma_start(out=bias[:, :, : E + 1], in_=b.rearrange("(h p) e -> p h e", p=P))
+            if e == 3:
+                rows = gate[:, 0, :].rearrange("r (c t) -> c r t", t=P)
+                nc.sync.dma_start(out=gate_rows[: TOP * T // P, :], in_=rows)
+                spread_gate()
+            if e in (4, 5):
+                for r in (2 * e - 8, 2 * e - 7):
+                    nc.sync.dma_start(out=pos_sb[r][:], in_=(pos1, pos2, pos3, pos4)[r])
+            return prepared
 
-        spread_gate()
         both = tuple(range(HALVES))
         for e0 in range(0, 16, 4):
             routed_run(tuple(range(e0, e0 + 4)), both, early, e0 // 2 % 4)

@@ -295,7 +295,7 @@ def tile_moe_shr_lin_bias_kernel(
         for o in range(PASSES):
             nc.sync.dma_start(out=words[o][:, :T], in_=x_words[o].rearrange("p t r -> p (t r)").bitcast(I32))
         for q in range(4):
-            nc.scalar.dma_start(
+            nc.gpsimd.dma_start(
                 out=planes[32 * q : 32 * q + 4 * PASSES, :T].bitcast(I32),
                 in_=x_scales[:, 4 * q : 4 * q + 4, :].bitcast(I32),
             )

@@ -33,7 +33,7 @@ WHOLE_SCALAR_COLS = 200
 BANK_BYTES = 2048
 BY_PASS = 17
 LATE_VECTOR_COLS = 96
-THROUGH = 3 * P
+THROUGH = 2 * P
 PIECES = (((0, 4 * P), (4 * P, P)), ((0, THROUGH),))
 
 
@@ -192,7 +192,7 @@ def tile_moe_shr_lin_bias_kernel(
         def shared_expert():
             raws = [load_pass(SHARED, o, 0, N) for o in range(PASSES)]
             codes, scales, stage = mx_tiles(N)
-            layout = ((4, (0, 1), N), (5, (2,), N), (6, (3, 4), P))
+            layout = ((4, (0, 1), N), (5, (2, 3, 4), P))
             accs = [bank(number, [P, len(chunks), width]) for number, chunks, width in layout]
             rows = bank(7, [P, T - THROUGH])
             for o in range(PASSES):
@@ -216,7 +216,16 @@ def tile_moe_shr_lin_bias_kernel(
                             start=(o == 0 and i == 0),
                             stop=(o == PASSES - 1 and i == len(chunks) - 1),
                         )
-                product(rows[:], codes, scales, N, 1, words, planes, THROUGH, T - THROUGH, (o,))
+                for t0, count in ((THROUGH, 2 * P), (THROUGH + 2 * P, P)):
+                    nc.tensor.matmul_mx(
+                        out=rows[:, t0 - THROUGH : t0 - THROUGH + count],
+                        lhsT=codes[:, o * N + P : (o + 1) * N].bitcast(FP8X4),
+                        lhsT_scale=scales[:, o * N + P : (o + 1) * N],
+                        rhs=words[o][:, t0 : t0 + count].bitcast(FP8X4),
+                        rhs_scale=planes[4 * o :, t0 : t0 + count],
+                        start=(o == 0 and t0 == THROUGH),
+                        stop=(o == PASSES - 1 and t0 > THROUGH),
+                    )
             for acc, (number, chunks, width) in zip(accs, layout):
                 nc.scalar.copy(out=ys_turned[:, chunks[0] : chunks[-1] + 1, :width], in_=acc[:])
             return rows

@@ -49,7 +49,7 @@ def tile_moe_shr_lin_bias_kernel(
 
         offs_sb = keep.tile([P, SLOTS // 16], U16, name="offs_sb")
         pos_sb = [keep.tile([P, T // 16], U16, name="pos_sb%d" % r) for r in range(TOP)]
-        words = [keep.tile([P, WINDOW], I32, name="words%d" % o, align_bytes=64) for o in range(PASSES)]
+        words = [keep.tile([P, WINDOW], I32, name="words%d" % o, align_bytes=256) for o in range(PASSES)]
         planes = keep.tile([P, WINDOW], U8, name="planes", align_bytes=64)
         bias = keep.tile([P, HALVES, 24], F32, name="bias")
         gate_rows = keep.tile([P, P], F32, name="gate_rows")
@@ -77,7 +77,7 @@ def tile_moe_shr_lin_bias_kernel(
             size = 4 * shape[1] * shape[2]
             start = landed[-1] if landed[-1] + size <= LANDING_BYTES else 0
             landed.append(start + size)
-            return landing.tile(shape, F32, name=name, offset=start)
+            return landing.tile(shape, F32, name=name, offset=start, align_bytes=256)
 
         def load_whole(e):
             raw = landing_tile([P, PASSES, PACK * N], "raw%d" % e)

@@ -1,3 +1,4 @@
+import math
 from contextlib import ExitStack
 
 import concourse.mybir as mybir
@@ -26,15 +27,20 @@ HALVES = N // P
 SLOTS = E * C
 SHARED = E
 GATHER = 512
+RUN = 4
 WINDOW = 704
+BUS = 256
 EXPERT_BYTES = 4 * PASSES * PACK * N
 LANDING_BYTES = 7 * EXPERT_BYTES
-WHOLE_SCALAR_COLS = 200
 BANK_BYTES = 2048
-BY_PASS = 17
-LATE_VECTOR_COLS = 96
-THROUGH = 2 * P
-PIECES = (((0, 4 * P), (4 * P, P)), ((0, THROUGH),))
+EARLY_CODES = {"0": 2}
+WHOLE = 8
+THROUGH = 3 * P
+SCALAR_ALONE = (9, 10, 11, 12, 14, 16)
+TERM_HOSTS = (9, 11, 13)
+SLOT_GROUPS = 3
+SLOT_BYTES = 4 * PASSES * GATHER
+TOKEN_PIECES = ((0, 4 * P), (4 * P, P))
 
 
 def tile_moe_shr_lin_bias_kernel(
@@ -45,11 +51,16 @@ def tile_moe_shr_lin_bias_kernel(
         keep = ctx.enter_context(tc.tile_pool(name="keep", bufs=1))
         ring = ctx.enter_context(tc.tile_pool(name="ring", bufs=2))
         landing = ctx.enter_context(tc.tile_pool(name="landing", bufs=1))
+        stages = ctx.enter_context(tc.tile_pool(name="stages", bufs=1))
+        code_pool = ctx.enter_context(tc.tile_pool(name="code_pool", bufs=1))
+        scale_pool = ctx.enter_context(tc.tile_pool(name="scale_pool", bufs=1))
+        slot_pool = ctx.enter_context(tc.tile_pool(name="slot_pool", bufs=1))
         psum = ctx.enter_context(tc.psum_pool(name="psum", bufs=1))
 
         offs_sb = keep.tile([P, SLOTS // 16], U16, name="offs_sb")
         pos_sb = [keep.tile([P, T // 16], U16, name="pos_sb%d" % r) for r in range(TOP)]
-        words = [keep.tile([P, WINDOW], I32, name="words%d" % o, align_bytes=256) for o in range(PASSES)]
+        all_words = keep.tile([P, PASSES, WINDOW], I32, name="all_words", align_bytes=BUS)
+        words = [all_words[:, o, :] for o in range(PASSES)]
         planes = keep.tile([P, WINDOW], U8, name="planes", align_bytes=64)
         bias = keep.tile([P, HALVES, 24], F32, name="bias")
         gate_rows = keep.tile([P, P], F32, name="gate_rows")
@@ -57,12 +68,10 @@ def tile_moe_shr_lin_bias_kernel(
         gate_sb = keep.tile([P, TOP, T], F32, name="gate_sb")
         ident = keep.tile([P, P], F32, name="ident")
         y = [keep.tile([P, SLOTS], F32, name="y%d" % h) for h in range(HALVES)]
-        ys_turned = keep.tile([P, T // P, N], F32, name="ys_turned")
 
         nc.vector.memset(planes[:].bitcast(I32), 0)
-        for o in range(PASSES):
-            nc.vector.memset(words[o][:, T:], 0)
-        nc.gpsimd.memset(gate_rows[:], 0.0)
+        nc.vector.memset(gate_rows[:], 0.0)
+        nc.vector.memset(all_words[:, :, T:], 0)
         make_identity(nc, ident[:])
 
         banks_taken = []
@@ -71,164 +80,175 @@ def tile_moe_shr_lin_bias_kernel(
             banks_taken.append(number)
             return psum.tile(shape, F32, name="bank%d" % len(banks_taken), offset=number * BANK_BYTES)
 
-        landed = [0]
+        places = {}
+
+        def ring_of_bytes(pool, size, align):
+            ends = [0]
+
+            def take(shape, dtype, item, name):
+                need = item * math.prod(shape[1:])
+                start = ends[-1] if ends[-1] + need <= size else 0
+                ends.append(start + need)
+                places.setdefault(name, start)
+                return pool.tile(shape, dtype, name=name, offset=start, align_bytes=align)
+
+            return take
+
+        take_landing = ring_of_bytes(landing, LANDING_BYTES, BUS)
+        take_stage = ring_of_bytes(stages, 5 * EXPERT_BYTES // 2, 64)
+        take_codes = ring_of_bytes(code_pool, 5 * EXPERT_BYTES // 4, 64)
+        take_scales = ring_of_bytes(scale_pool, 5 * EXPERT_BYTES // 16, 64)
 
         def landing_tile(shape, name):
-            size = 4 * shape[1] * shape[2]
-            start = landed[-1] if landed[-1] + size <= LANDING_BYTES else 0
-            landed.append(start + size)
-            return landing.tile(shape, F32, name=name, offset=start, align_bytes=256)
+            return take_landing(shape, F32, 4, name)
 
-        def load_whole(e):
-            raw = landing_tile([P, PASSES, PACK * N], "raw%d" % e)
-            nc.sync.dma_start(out=raw[:], in_=w[e].rearrange("(o p j) n -> p o (j n)", p=P, j=PACK))
-            return raw[:].rearrange("p o (j n) -> p o j n", j=PACK)
-
-        def load_pass(e, o, first, width):
-            raw = landing_tile([P, PACK, width], "raw%d_%d_%d" % (e, first, o))
+        def pass_rows(e, o, first, width):
             rows = w[e, o * P * PACK : (o + 1) * P * PACK, first : first + width]
-            nc.sync.dma_start(out=raw[:], in_=rows.rearrange("(p j) n -> p j n", j=PACK))
-            return raw[:]
+            return rows.rearrange("(p j) n -> p j n", j=PACK)
 
-        def mx_tiles(width):
-            codes = ring.tile([P, PASSES * width], U32, name="codes", bufs=6, align_bytes=64)
-            scales = ring.tile([P, PASSES * width], U8, name="scales", bufs=6, align_bytes=64)
-            stage = ring.tile([P, PASSES * PACK * width], BF16, name="stage", bufs=4, align_bytes=64)
+        def mx_tiles(width, name):
+            if name in EARLY_CODES:
+                start = EARLY_CODES[name] * SLOT_BYTES
+                codes = slot_pool.tile([P, PASSES * width], U32, name="codes" + name, offset=start, align_bytes=64)
+            elif name == "shared":
+                start = places["codes19_1"] + 4 * P
+                codes = code_pool.tile([P, PASSES * width], U32, name="codes_shared", offset=start, align_bytes=64)
+            else:
+                codes = take_codes([P, PASSES * width], U32, 4, "codes" + name)
+            scales = take_scales([P, PASSES * width], U8, 1, "scales" + name)
+            if name == "shared":
+                stage = [take_stage([P, PACK * width], BF16, 2, "stage_shared0")]
+                for o in (1, 2):
+                    start = places["stage19_1"] + PACK * P + 2 * PACK * N * (o - 1)
+                    stage.append(
+                        stages.tile([P, PACK * width], BF16, name="stage_shared%d" % o, offset=start, align_bytes=64)
+                    )
+            else:
+                stage = take_stage([P, PASSES * PACK * width], BF16, 2, "stage" + name)
             return codes, scales, stage
 
-        def quantize(codes, scales, stage, width):
-            for a, z in ((0, 2 * width), (2 * width, 3 * width)):
-                nc.vector.quantize_mx(
-                    out=codes[:, a:z].bitcast(FP8X4), scales=scales[:, a:z], in_=stage[:, PACK * a : PACK * z]
+        def quantize(codes, scales, stage, a, z):
+            nc.vector.quantize_mx(
+                out=codes[:, a:z].bitcast(FP8X4), scales=scales[:, a:z], in_=stage[:, PACK * a : PACK * z]
+            )
+
+        def round_rows(raw, flat, engine):
+            if engine == "gpsimd":
+                nc.gpsimd.tensor_scalar(
+                    out=flat.rearrange("p (o n j) -> p o n j", o=raw.shape[1], j=PACK),
+                    in0=raw.rearrange("p o j n -> p o n j"),
+                    scalar1=1.0, scalar2=0.0, op0=MULT, op1=ADD,
                 )
-            return codes, scales
+                return
+            dst = flat.rearrange("p (o c i j) -> p o c j i", o=raw.shape[1], i=4, j=PACK)
+            src = raw.rearrange("p o j (c i) -> p o c j i", i=4)
+            if engine == "scalar":
+                nc.scalar.copy(out=dst, in_=src)
+            else:
+                nc.vector.tensor_copy(out=dst, in_=src)
 
         def whole_expert(e):
-            raws = load_whole(e)
-            codes, scales, stage = mx_tiles(N)
-            dst = stage[:].rearrange("p (o c i j) -> p c o j i", o=PASSES, i=4, j=PACK)
-            src = raws.rearrange("p o j (c i) -> p c o j i", i=4)
-            cut = WHOLE_SCALAR_COLS // 4
-            nc.scalar.copy(out=dst[:, :cut], in_=src[:, :cut])
-            nc.vector.tensor_copy(out=dst[:, cut:], in_=src[:, cut:])
-            return quantize(codes, scales, stage, N)
+            raw = landing_tile([P, PASSES, PACK * N], "raw%d" % e)
+            nc.sync.dma_start(out=raw[:], in_=w[e].rearrange("(o p j) n -> p o (j n)", p=P, j=PACK))
+            codes, scales, stage = mx_tiles(N, "%d" % e)
+            view = raw[:].rearrange("p o (j n) -> p o j n", j=PACK)
+            round_rows(view[:, :2], stage[:, : 2 * PACK * N], "scalar")
+            round_rows(view[:, 2:], stage[:, 2 * PACK * N :], "gpsimd")
+            quantize(codes, scales, stage, 0, 2 * N)
+            quantize(codes, scales, stage, 2 * N, 3 * N)
+            return codes, scales
 
-        def late_expert(e):
-            raws = [load_pass(e, o, 0, N) for o in range(PASSES)]
-            codes, scales, stage = mx_tiles(N)
+        def half_expert(e, h):
+            raws = [landing_tile([P, PACK, P], "raw%d_%d_%d" % (e, h, o))[:] for o in range(PASSES)]
             for o in range(PASSES):
-                final = (e, o) == (E - 1, PASSES - 1)
-                cut = (P if final else LATE_VECTOR_COLS) // 4
-                dst = stage[:, PACK * o * N : PACK * (o + 1) * N].rearrange("p (c i j) -> p c j i", i=4, j=PACK)
-                src = raws[o].rearrange("p j (c i) -> p c j i", i=4)
-                nc.vector.tensor_copy(out=dst[:, :cut], in_=src[:, :cut])
-                nc.scalar.copy(out=dst[:, cut:], in_=src[:, cut:])
-                width = P if final else N
-                for first in range(o * N, (o + 1) * N, width):
-                    cols = slice(first, first + width)
-                    flat = stage[:, PACK * first : PACK * (first + width)]
-                    nc.vector.quantize_mx(out=codes[:, cols].bitcast(FP8X4), scales=scales[:, cols], in_=flat)
+                nc.sync.dma_start(out=raws[o], in_=pass_rows(e, o, h * P, P))
+            codes, scales, stage = mx_tiles(P, "%d_%d" % (e, h))
+            if e == E - 1:
+                third = "vector"
+            elif h == 1:
+                third = "scalar" if e in SCALAR_ALONE else "vector"
+            else:
+                third = "gpsimd"
+            for o, engine in enumerate(("scalar", "scalar", third)):
+                round_rows(raws[o].unsqueeze(1), stage[:, PACK * o * P : PACK * (o + 1) * P], engine)
+            if e == E - 1:
+                quantize(codes, scales, stage, 0, 2 * P)
+                quantize(codes, scales, stage, 2 * P, 3 * P)
+            else:
+                quantize(codes, scales, stage, 0, PASSES * P)
             return codes, scales
 
         def gather_tokens(g):
-            slot_words = ring.tile([P, PASSES * GATHER], U32, name="slot_words", bufs=3, align_bytes=64)
-            slot_planes = ring.tile([P, GATHER], U8, name="slot_planes", bufs=3, align_bytes=64)
+            slot_words = slot_pool.tile(
+                [P, PASSES * GATHER], U32, name="slot_words%d" % g, offset=g % SLOT_GROUPS * SLOT_BYTES, align_bytes=64
+            )
+            slot_planes = ring.tile([P, GATHER], U8, name="slot_planes", bufs=SLOT_GROUPS, align_bytes=64)
             entries = offs_sb[:, g * GATHER // 16 : (g + 1) * GATHER // 16]
             for o in range(PASSES):
-                window = words[o][:].bitcast(U32)
+                window = words[o].bitcast(U32)
                 nc.vector.tensor_copy(out=slot_words[:, o * GATHER : (o + 1) * GATHER], in_=window.indirect(entries))
             nc.vector.tensor_copy(out=slot_planes[:], in_=planes[:].indirect(entries))
-            return [slot_words[:, o * GATHER : (o + 1) * GATHER] for o in range(PASSES)], slot_planes
-
-        def product(acc, codes, scales, width, i, moving, moving_planes, first, count=P, passes=range(PASSES)):
-            for o in passes:
-                cols = slice(o * width + i * P, o * width + (i + 1) * P)
-                nc.tensor.matmul_mx(
-                    out=acc,
-                    lhsT=codes[:, cols].bitcast(FP8X4),
-                    lhsT_scale=scales[:, cols],
-                    rhs=moving[o][:, first : first + count].bitcast(FP8X4),
-                    rhs_scale=moving_planes[4 * o :, first : first + count],
-                    start=(o == 0),
-                    stop=(o == PASSES - 1),
-                )
+            return slot_words, slot_planes
 
         gathered = {}
 
-        def slots_of(e):
+        def product(acc, codes, scales, width, i, e, o):
             g, first = divmod(e * C, GATHER)
             if g not in gathered:
                 gathered.setdefault(g, gather_tokens(g))
-            return gathered[g] + (first,)
+            slot_words, slot_planes = gathered[g]
+            cols = slice(o * width + i * P, o * width + (i + 1) * P)
+            nc.tensor.matmul_mx(
+                out=acc,
+                lhsT=codes[:, cols].bitcast(FP8X4),
+                lhsT_scale=scales[:, cols],
+                rhs=slot_words[:, o * GATHER + first : o * GATHER + first + C].bitcast(FP8X4),
+                rhs_scale=slot_planes[4 * o :, first : first + C],
+                start=(o == 0),
+                stop=(o == PASSES - 1),
+            )
 
-        def routed_run(experts, halves, prepare, first_bank):
-            width = len(halves) * P
-            accs = [bank(first_bank + h, [P, len(experts) * C]) for h in halves]
-            for n, e in enumerate(experts):
-                codes, scales = prepare(e)
-                slots = slots_of(e)
-                if len(experts) == 1:
-                    for passes in ((0, 1), (2,)):
-                        for i in range(len(halves)):
-                            product(accs[i][:], codes, scales, width, i, *slots, passes=passes)
-                else:
-                    for i in range(len(halves)):
-                        product(accs[i][:, n * C : (n + 1) * C], codes, scales, width, i, *slots)
-            e0, count = experts[0], len(experts)
-            for acc, h in zip(accs, halves):
-                dst = y[h][:, e0 * C : (e0 + count) * C]
-                if e0 == E - 1 and h == 1:
-                    nc.scalar.activation(out=dst, in_=acc[:], func=IDENTITY, bias=bias[:, h, e0 : e0 + 1])
-                elif count == 1:
-                    nc.vector.tensor_scalar(out=dst, in0=acc[:], scalar1=bias[:, h, e0 : e0 + 1], scalar2=None, op0=ADD)
-                else:
-                    nc.vector.tensor_tensor(
-                        out=dst.rearrange("p (e c) -> p e c", c=C),
-                        in0=acc[:].rearrange("p (e c) -> p e c", c=C),
-                        in1=bias[:, h, e0 : e0 + count].unsqueeze(2).to_broadcast([P, count, C]),
-                        op=ADD,
-                    )
+        def add_bias(acc, h, e0, count):
+            nc.vector.tensor_tensor(
+                out=y[h][:, e0 * C : (e0 + count) * C].rearrange("p (e c) -> p e c", c=C),
+                in0=acc[:].rearrange("p (e c) -> p e c", c=C),
+                in1=bias[:, h, e0 : e0 + count].unsqueeze(2).to_broadcast([P, count, C]),
+                op=ADD,
+            )
 
-        def shared_expert():
-            raws = [load_pass(SHARED, o, 0, N) for o in range(PASSES)]
-            codes, scales, stage = mx_tiles(N)
-            layout = ((4, (0, 1), N), (5, (2, 3, 4), P))
-            accs = [bank(number, [P, len(chunks), width]) for number, chunks, width in layout]
-            rows = bank(7, [P, T - THROUGH])
-            for o in range(PASSES):
-                flat = stage[:, o * PACK * N : (o + 1) * PACK * N]
-                dst = flat.rearrange("p (c i j) -> p c j i", i=4, j=PACK)
-                src = raws[o].rearrange("p j (c i) -> p c j i", i=4)
-                if o < PASSES - 1:
-                    nc.scalar.copy(out=dst, in_=src)
-                else:
-                    nc.vector.tensor_copy(out=dst, in_=src)
-                cols = slice(o * N, (o + 1) * N)
-                nc.vector.quantize_mx(out=codes[:, cols].bitcast(FP8X4), scales=scales[:, cols], in_=flat)
-                for acc, (number, chunks, width) in zip(accs, layout):
-                    for i, c in enumerate(chunks):
-                        nc.tensor.matmul_mx(
-                            out=acc[:, i, :],
-                            lhsT=words[o][:, c * P : (c + 1) * P].bitcast(FP8X4),
-                            lhsT_scale=planes[4 * o :, c * P : (c + 1) * P],
-                            rhs=codes[:, o * N : o * N + width].bitcast(FP8X4),
-                            rhs_scale=scales[:, o * N : o * N + width],
-                            start=(o == 0 and i == 0),
-                            stop=(o == PASSES - 1 and i == len(chunks) - 1),
-                        )
-                for t0, count in ((THROUGH, 2 * P), (THROUGH + 2 * P, P)):
-                    nc.tensor.matmul_mx(
-                        out=rows[:, t0 - THROUGH : t0 - THROUGH + count],
-                        lhsT=codes[:, o * N + P : (o + 1) * N].bitcast(FP8X4),
-                        lhsT_scale=scales[:, o * N + P : (o + 1) * N],
-                        rhs=words[o][:, t0 : t0 + count].bitcast(FP8X4),
-                        rhs_scale=planes[4 * o :, t0 : t0 + count],
-                        start=(o == 0 and t0 == THROUGH),
-                        stop=(o == PASSES - 1 and t0 > THROUGH),
+        def small_loads(e):
+            if e == 2:
+                nc.sync.dma_start(out=bias[:, :, : E + 1], in_=b.rearrange("(h p) e -> p h e", p=P))
+            if e == 0:
+                for q in range(4):
+                    nc.sync.dma_start(
+                        out=planes[32 * q : 32 * q + 4 * PASSES, :T].bitcast(I32),
+                        in_=x_scales[:, 4 * q : 4 * q + 4, :].bitcast(I32),
                     )
-            for acc, (number, chunks, width) in zip(accs, layout):
-                nc.scalar.copy(out=ys_turned[:, chunks[0] : chunks[-1] + 1, :width], in_=acc[:])
-            return rows
+            if e in (4, 5):
+                for r in (2 * e - 8, 2 * e - 7):
+                    nc.sync.dma_start(out=pos_sb[r][:], in_=(pos1, pos2, pos3, pos4)[r])
+
+        def whole_run(e0, count, first_bank):
+            accs = [bank(first_bank + h, [P, count * C]) for h in range(HALVES)]
+            for n in range(count):
+                codes, scales = whole_expert(e0 + n)
+                small_loads(e0 + n)
+                for h in range(HALVES):
+                    for o in range(PASSES):
+                        product(accs[h][:, n * C : (n + 1) * C], codes, scales, N, h, e0 + n, o)
+            for h in range(HALVES):
+                add_bias(accs[h], h, e0, count)
+
+        def half_run(e0, count, h, number, after=None):
+            acc = bank(number, [P, count * C])
+            for n in range(count):
+                codes, scales = half_expert(e0 + n, h)
+                for o in range(PASSES):
+                    product(acc[:, n * C : (n + 1) * C], codes, scales, P, 0, e0 + n, o)
+                if after is not None:
+                    after(e0 + n)
+            add_bias(acc, h, e0, count)
 
         def spread_gate():
             turned = bank(4, [P, P])
@@ -243,118 +263,120 @@ def tile_moe_shr_lin_bias_kernel(
                     nc.tensor.transpose(back[:, i * P : (i + 1) * P], column, ident[:])
                 nc.scalar.copy(out=flat[:, first * P : (first + 4) * P], in_=back[:])
 
-        def add_back(h, sums, term, first):
-            for acc, (t0, count) in zip(sums, PIECES[h]):
-                for c in range(0, count, P):
-                    nc.tensor.matmul(
-                        acc[:, c : c + P], lhsT=term((t0 + c) // P), rhs=ident[:], is_transpose=True,
-                        start=(first and c == 0), stop=(not first and c == count - P),
-                    )
-
-        def open_sums(h):
-            sums = [bank(4 + 2 * h + i, [P, count]) for i, (t0, count) in enumerate(PIECES[h])]
-            add_back(h, sums, lambda c: ys_turned[:, c, h * P : (h + 1) * P], True)
-            return sums
+        def turn(sources, numbers, spans, dst):
+            accs = [bank(number, [P, count]) for number, (t0, count) in zip(numbers, spans)]
+            for r, source in enumerate(sources):
+                for acc, (t0, count) in zip(accs, spans):
+                    for c in range(0, count, P):
+                        nc.tensor.matmul(
+                            acc[:, c : c + P], lhsT=source[:, t0 + c : t0 + c + P], rhs=ident[:], is_transpose=True,
+                            start=(r == 0 and c == 0), stop=(r == len(sources) - 1 and c == count - P),
+                        )
+            if dst is not None:
+                for acc, (t0, count) in zip(accs, spans):
+                    nc.scalar.copy(out=dst[:, t0 : t0 + count], in_=acc[:])
+            return accs
 
         def fetched(h, r, t0, count):
             return y[h][:].indirect(pos_sb[r][:, t0 // 16 : (t0 + count) // 16])
 
-        def fetch_plain(h, lists, t0, count, tag):
-            plain = keep.tile([P, len(lists), count], F32, name="plain%d_%d" % (h, t0), tag=tag)
-            for i, r in enumerate(lists):
-                nc.scalar.activation(out=plain[:, i, :], in_=fetched(h, r, t0, count), func=COPY)
-            return plain
-
-        def fetch_weighed(h, lists, t0, count, tag):
-            products = keep.tile([P, len(lists), count], F32, name="fetched%d_%d" % (h, lists[0]), tag=tag)
-            for i, r in enumerate(lists):
-                nc.vector.tensor_tensor(
-                    out=products[:, i, :], in0=fetched(h, r, t0, count), in1=gate_sb[:, r, t0 : t0 + count], op=MULT
-                )
-            return [products[:, i, :] for i in range(len(lists))]
-
-        def weigh(h, plain, lists, t0, count):
-            products = keep.tile([P, len(lists), count], F32, name="weighed%d_%d" % (h, t0))
-            weights = gate_sb[:, lists[0] : lists[-1] + 1, t0 : t0 + count]
-            nc.vector.tensor_tensor(out=products[:], in0=plain[:], in1=weights, op=MULT)
-            return [products[:, i, :] for i in range(len(lists))]
-
-        def add_up(h, products):
-            total = keep.tile([P, products[0].shape[1]], F32, name="total%d" % h)
-            result = keep.tile([P, products[0].shape[1]], F32, name="result%d" % h)
-            turned = [bank(2 * h + i, [P, count]) for i, (t0, count) in enumerate(PIECES[h])]
-            for r in range(TOP):
-                for acc, (t0, count) in zip(turned, PIECES[h]):
-                    for c in range(0, count, P):
-                        nc.tensor.matmul(
-                            acc[:, c : c + P], lhsT=products[r][:, t0 + c : t0 + c + P], rhs=ident[:],
-                            is_transpose=True, start=(r == 0 and c == 0), stop=(r == TOP - 1 and c == count - P),
-                        )
-            for acc, (t0, count) in zip(turned, PIECES[h]):
-                nc.scalar.copy(out=total[:, t0 : t0 + count], in_=acc[:])
-            sums = open_sums(h)
-            add_back(h, sums, lambda c: total[:, c * P : (c + 1) * P], False)
-            for acc, (t0, count) in zip(sums, PIECES[h]):
-                nc.scalar.activation(
-                    out=result[:, t0 : t0 + count], in_=acc[:], func=IDENTITY, bias=bias[:, h, SHARED : SHARED + 1]
-                )
-            nc.scalar.dma_start(out=out[h * P : (h + 1) * P, : products[0].shape[1]], in_=result[:])
+        def fetch_weighed(h, r, dst, t0, count):
+            nc.vector.tensor_tensor(out=dst, in0=fetched(h, r, t0, count), in1=gate_sb[:, r, t0 : t0 + count], op=MULT)
 
         nc.sync.dma_start(out=offs_sb[:], in_=offs)
+        nc.sync.dma_start(out=all_words[:, :, :T], in_=x_words.rearrange("o p t r -> p o (t r)").bitcast(I32))
+        rows = gate[:, 0, :].rearrange("r (c t) -> c r t", t=P)
+        nc.scalar.dma_start(out=gate_rows[: TOP * T // P, :], in_=rows)
+        spread_gate()
+
+        def behind(host, count, name):
+            return landing.tile([P, count], F32, name=name, offset=places[host], align_bytes=BUS)
+
+        for i, e0 in enumerate(range(0, WHOLE, RUN)):
+            whole_run(e0, min(RUN, WHOLE - e0), 2 * (i % 2))
+        for e0 in range(WHOLE, E, RUN):
+            half_run(e0, RUN, 0, e0 // RUN % 2)
+        terms = [keep.tile([P, T], F32, name="term0")]
+        fetch_weighed(0, 0, terms[0][:], 0, T)
+
+        def next_term(e):
+            if e in TERM_HOSTS:
+                terms.append(behind("raw%d_1_1" % e, T, "term%d" % e))
+                fetch_weighed(0, len(terms) - 1, terms[-1][:], 0, T)
+
+        for e0 in range(WHOLE, E, RUN):
+            half_run(e0, RUN, 1, 2 + e0 // RUN % 2, next_term)
+        total = behind("raw19_1_0", T, "total")
+        turn(terms, (4, 5), TOKEN_PIECES, total)
+
+        raws = []
         for o in range(PASSES):
-            nc.sync.dma_start(out=words[o][:, :T], in_=x_words[o].rearrange("p t r -> p (t r)").bitcast(I32))
-        for q in range(4):
-            nc.gpsimd.dma_start(
-                out=planes[32 * q : 32 * q + 4 * PASSES, :T].bitcast(I32),
-                in_=x_scales[:, 4 * q : 4 * q + 4, :].bitcast(I32),
+            raw = landing_tile([P, PACK, N], "shared%d" % o)
+            nc.sync.dma_start(out=raw[:], in_=pass_rows(SHARED, o, 0, N))
+            raws.append(raw)
+        codes, scales, stage = mx_tiles(N, "shared")
+        pieces = ((0, 0, 4 * P), (0, 4 * P, P), (1, 0, 2 * P), (1, 2 * P, P), (1, THROUGH, T - THROUGH))
+        long_sums = bank(0, [P, 4 * P])
+        mixed_sums = bank(1, [P, 4 * P])
+        last_sums = bank(6, [P, T - THROUGH])
+        homes = (long_sums[:], mixed_sums[:, :P], mixed_sums[:, P : 3 * P], mixed_sums[:, 3 * P :], last_sums[:])
+
+        def shared_pass(o):
+            round_rows(raws[o][:].unsqueeze(1), stage[o][:], "scalar")
+            span = slice(o * N, (o + 1) * N)
+            nc.vector.quantize_mx(out=codes[:, span].bitcast(FP8X4), scales=scales[:, span], in_=stage[o][:])
+            for i, (h, t0, count) in enumerate(pieces):
+                cols = slice(o * N + h * P, o * N + (h + 1) * P)
+                nc.tensor.matmul_mx(
+                    out=homes[i],
+                    lhsT=codes[:, cols].bitcast(FP8X4),
+                    lhsT_scale=scales[:, cols],
+                    rhs=words[o][:, t0 : t0 + count].bitcast(FP8X4),
+                    rhs_scale=planes[4 * o :, t0 : t0 + count],
+                    start=(o == 0 and i in (0, 1, 4)),
+                    stop=(o == PASSES - 1 and i in (0, 3, 4)),
+                )
+
+        def add_shared(h, sums, routed, dst):
+            nc.vector.scalar_tensor_tensor(
+                out=dst, in0=sums, scalar=bias[:, h, SHARED : SHARED + 1], in1=routed, op0=ADD, op1=ADD
             )
 
-        def early(e):
-            if e >= BY_PASS:
-                return late_expert(e)
-            prepared = whole_expert(e)
-            if e == 2:
-                nc.sync.dma_start(out=bias[:, :, : E + 1], in_=b.rearrange("(h p) e -> p h e", p=P))
-            if e == 3:
-                rows = gate[:, 0, :].rearrange("r (c t) -> c r t", t=P)
-                nc.sync.dma_start(out=gate_rows[: TOP * T // P, :], in_=rows)
-                spread_gate()
-            if e in (4, 5):
-                for r in (2 * e - 8, 2 * e - 7):
-                    nc.sync.dma_start(out=pos_sb[r][:], in_=(pos1, pos2, pos3, pos4)[r])
-            return prepared
-
-        both = tuple(range(HALVES))
-        for e0 in range(0, 16, 4):
-            routed_run(tuple(range(e0, e0 + 4)), both, early, e0 // 2 % 4)
-        routed_run((16, 17), both, early, 0)
-        routed_run((18,), both, early, 2)
-        routed_run((19,), both, early, 0)
-        shared_rows = shared_expert()
-
         rest = T - THROUGH
-        plain = fetch_plain(0, (2, 3), 0, T, "first_plain")
-        first = fetch_weighed(0, (0, 1), 0, T, "first_fetched") + weigh(0, plain, (2, 3), 0, T)
-        plain = fetch_plain(1, (3,), 0, THROUGH, "second_plain")
-        second = fetch_weighed(1, (0,), 0, THROUGH, "second_fetched")
-        second = second + fetch_weighed(1, (1, 2), 0, THROUGH, "first_plain") + weigh(1, plain, (3,), 0, THROUGH)
-        add_up(0, first)
-        add_up(1, second)
-
-        plain = fetch_plain(1, (3,), THROUGH, rest, "last_plain")
-        last = weigh(1, plain, (3,), THROUGH, rest)
-        products = keep.tile([P, TOP - 1, rest], F32, name="last_fetched", tag="second_plain")
-        steps = keep.tile([P, TOP, rest], F32, name="steps")
-        for r in range(TOP):
-            if r < TOP - 1:
-                nc.vector.tensor_tensor(
-                    out=products[:, r, :], in0=fetched(1, r, THROUGH, rest), in1=gate_sb[:, r, THROUGH:], op=MULT
-                )
-            if r == 0:
-                nc.vector.scalar_tensor_tensor(
-                    out=steps[:, 0, :], in0=shared_rows[:], scalar=bias[:, 1, SHARED : SHARED + 1],
-                    in1=last[0], op0=ADD, op1=ADD,
-                )
-            else:
-                nc.vector.tensor_tensor(out=steps[:, r, :], in0=steps[:, r - 1, :], in1=products[:, r - 1, :], op=ADD)
-        nc.sync.dma_start(out=out[P:, THROUGH:], in_=steps[:, 3, :])
+        plain = keep.tile([P, THROUGH], F32, name="plain")
+        plain_rest = keep.tile([P, 2, rest], F32, name="plain_rest")
+        results = [keep.tile([P, T], F32, name="result%d" % h, align_bytes=BUS) for h in range(HALVES)]
+        for o in range(PASSES):
+            shared_pass(o)
+        late_terms = [keep.tile([P, T], F32, name="late0"), behind("shared0", T, "late1")]
+        late_terms = late_terms + [behind("shared2", THROUGH, "late2"), keep.tile([P, THROUGH], F32, name="late3")]
+        rest_terms = keep.tile([P, 2, rest], F32, name="rest_terms")
+        nc.scalar.activation(out=plain[:], in_=fetched(1, 3, 0, THROUGH), func=COPY)
+        for r in (2, 3):
+            nc.scalar.activation(out=plain_rest[:, r - 2, :], in_=fetched(1, r, THROUGH, rest), func=COPY)
+        routed0 = behind("shared1", T, "routed0")
+        turn([total], (3, 7), TOKEN_PIECES, routed0)
+        for r in (0, 1):
+            fetch_weighed(1, r, late_terms[r][:], 0, T)
+        fetch_weighed(1, 2, late_terms[2][:], 0, THROUGH)
+        nc.vector.tensor_tensor(out=late_terms[3][:], in0=plain[:], in1=gate_sb[:, 3, :THROUGH], op=MULT)
+        late_total = keep.tile([P, THROUGH], F32, name="late_total")
+        routed1 = keep.tile([P, rest], F32, name="routed1")
+        shared1 = keep.tile([P, THROUGH], F32, name="shared1")
+        nc.scalar.activation(out=shared1[:], in_=mixed_sums[:, P:], func=IDENTITY, bias=bias[:, 1, SHARED : SHARED + 1])
+        turn(late_terms, (5,), ((0, THROUGH),), late_total)
+        (turned_back,) = turn([late_total], (4,), ((0, THROUGH),), None)
+        steps = keep.tile([P, 2, rest], F32, name="steps")
+        nc.vector.tensor_tensor(
+            out=steps[:, 0, :], in0=late_terms[0][:, THROUGH:], in1=late_terms[1][:, THROUGH:], op=ADD
+        )
+        nc.vector.tensor_tensor(out=rest_terms[:], in0=plain_rest[:], in1=gate_sb[:, 2:, THROUGH:], op=MULT)
+        nc.vector.tensor_tensor(out=steps[:, 1, :], in0=steps[:, 0, :], in1=rest_terms[:, 0, :], op=ADD)
+        add_shared(0, homes[0], routed0[:, : 4 * P], results[0][:, : 4 * P])
+        nc.vector.tensor_tensor(out=routed1[:], in0=steps[:, 1, :], in1=rest_terms[:, 1, :], op=ADD)
+        add_shared(0, homes[1], routed0[:, 4 * P :], results[0][:, 4 * P :])
+        nc.sync.dma_start(out=out[:P, :], in_=results[0][:])
+        add_shared(1, last_sums[:], routed1[:], results[1][:, THROUGH:])
+        nc.scalar.dma_start(out=out[P:, THROUGH:], in_=results[1][:, THROUGH:])
+        nc.vector.tensor_tensor(out=results[1][:, :THROUGH], in0=turned_back[:], in1=shared1[:], op=ADD)
+        nc.sync.dma_start(out=out[P:, :THROUGH], in_=results[1][:, :THROUGH])

@@ -1,4 +1,3 @@
-import math
 from contextlib import ExitStack
 
 import concourse.mybir as mybir
@@ -30,17 +29,27 @@ GATHER = 512
 RUN = 4
 WINDOW = 704
 BUS = 256
-EXPERT_BYTES = 4 * PASSES * PACK * N
-LANDING_BYTES = 7 * EXPERT_BYTES
-BANK_BYTES = 2048
-EARLY_CODES = {"0": 2}
-WHOLE = 8
-THROUGH = 3 * P
-SCALAR_ALONE = (9, 10, 11, 12, 14, 16)
-TERM_HOSTS = (9, 11, 13)
+KIB = 1024
+BANK_BYTES = 2 * KIB
+WHOLE = 10
+WHOLE_RUNS = ((0, 4), (4, 4), (8, 2))
+HALF_RUNS = ((10, 4), (14, 4), (18, 2))
+FIRST_BANKS = (2, 3, 0)
+SECOND_BANKS = (2, 3, 1)
+DEPTH = 5
+LAST_SLOT = 2
+SCALAR_ALONE = ((10, 12, 14, 16), (10, 11, 12, 13, 14, 15))
+VECTOR_STAGE = 30 * KIB
+SCALAR_COLUMNS = 96
+LAST_AT = 3 * KIB // 2
+HALF_WORDS = PASSES * P
+LANDING_BYTES = 84 * KIB
 SLOT_GROUPS = 3
 SLOT_BYTES = 4 * PASSES * GATHER
+THROUGH = 3 * P
 TOKEN_PIECES = ((0, 4 * P), (4 * P, P))
+HALF_CODES = (0, 3 * KIB // 2, 9 * KIB, 21 * KIB // 2)
+HALF_SCALES = (1536, 1920, 768, 1152)
 
 
 def tile_moe_shr_lin_bias_kernel(
@@ -49,7 +58,7 @@ def tile_moe_shr_lin_bias_kernel(
     nc = tc.nc
     with ExitStack() as ctx:
         keep = ctx.enter_context(tc.tile_pool(name="keep", bufs=1))
-        ring = ctx.enter_context(tc.tile_pool(name="ring", bufs=2))
+        ring = ctx.enter_context(tc.tile_pool(name="ring", bufs=SLOT_GROUPS))
         landing = ctx.enter_context(tc.tile_pool(name="landing", bufs=1))
         stages = ctx.enter_context(tc.tile_pool(name="stages", bufs=1))
         code_pool = ctx.enter_context(tc.tile_pool(name="code_pool", bufs=1))
@@ -80,133 +89,66 @@ def tile_moe_shr_lin_bias_kernel(
             banks_taken.append(number)
             return psum.tile(shape, F32, name="bank%d" % len(banks_taken), offset=number * BANK_BYTES)
 
-        places = {}
-
-        def ring_of_bytes(pool, size, align):
-            ends = [0]
-
-            def take(shape, dtype, item, name):
-                need = item * math.prod(shape[1:])
-                start = ends[-1] if ends[-1] + need <= size else 0
-                ends.append(start + need)
-                places.setdefault(name, start)
-                return pool.tile(shape, dtype, name=name, offset=start, align_bytes=align)
-
-            return take
-
-        take_landing = ring_of_bytes(landing, LANDING_BYTES, BUS)
-        take_stage = ring_of_bytes(stages, 5 * EXPERT_BYTES // 2, 64)
-        take_codes = ring_of_bytes(code_pool, 5 * EXPERT_BYTES // 4, 64)
-        take_scales = ring_of_bytes(scale_pool, 5 * EXPERT_BYTES // 16, 64)
+        landed_at = {}
+        landing_ends = [0]
 
         def landing_tile(shape, name):
-            return take_landing(shape, F32, 4, name)
+            need = 4 * shape[1] * shape[2]
+            start = landing_ends[-1] if landing_ends[-1] + need <= LANDING_BYTES else 0
+            landing_ends.append(start + need)
+            landed_at.setdefault(name, start)
+            return landing.tile(shape, F32, name=name, offset=start, align_bytes=BUS)
 
-        def pass_rows(e, o, first, width):
-            rows = w[e, o * P * PACK : (o + 1) * P * PACK, first : first + width]
-            return rows.rearrange("(p j) n -> p j n", j=PACK)
+        def placed(pool, count, dtype, name, offset):
+            return pool.tile([P, count], dtype, name=name, offset=offset, align_bytes=64)
 
-        def mx_tiles(width, name):
-            if name in EARLY_CODES:
-                start = EARLY_CODES[name] * SLOT_BYTES
-                codes = slot_pool.tile([P, PASSES * width], U32, name="codes" + name, offset=start, align_bytes=64)
-            elif name == "shared":
-                start = places["codes19_1"] + 4 * P
-                codes = code_pool.tile([P, PASSES * width], U32, name="codes_shared", offset=start, align_bytes=64)
-            else:
-                codes = take_codes([P, PASSES * width], U32, 4, "codes" + name)
-            scales = take_scales([P, PASSES * width], U8, 1, "scales" + name)
-            if name == "shared":
-                stage = [take_stage([P, PACK * width], BF16, 2, "stage_shared0")]
-                for o in (1, 2):
-                    start = places["stage19_1"] + PACK * P + 2 * PACK * N * (o - 1)
-                    stage.append(
-                        stages.tile([P, PACK * width], BF16, name="stage_shared%d" % o, offset=start, align_bytes=64)
-                    )
-            else:
-                stage = take_stage([P, PASSES * PACK * width], BF16, 2, "stage" + name)
-            return codes, scales, stage
+        def on_landing(host, count, name):
+            return landing.tile([P, count], F32, name=name, offset=landed_at[host], align_bytes=BUS)
 
-        def quantize(codes, scales, stage, a, z):
-            nc.vector.quantize_mx(
-                out=codes[:, a:z].bitcast(FP8X4), scales=scales[:, a:z], in_=stage[:, PACK * a : PACK * z]
-            )
-
-        def round_rows(raw, flat, engine):
+        def round_rows(raw, stage, engine):
             if engine == "gpsimd":
                 nc.gpsimd.tensor_scalar(
-                    out=flat.rearrange("p (o n j) -> p o n j", o=raw.shape[1], j=PACK),
+                    out=stage.rearrange("p (o n j) -> p o n j", o=raw.shape[1], j=PACK),
                     in0=raw.rearrange("p o j n -> p o n j"),
                     scalar1=1.0, scalar2=0.0, op0=MULT, op1=ADD,
                 )
                 return
-            dst = flat.rearrange("p (o c i j) -> p o c j i", o=raw.shape[1], i=4, j=PACK)
+            dst = stage.rearrange("p (o c i j) -> p o c j i", o=raw.shape[1], i=4, j=PACK)
             src = raw.rearrange("p o j (c i) -> p o c j i", i=4)
             if engine == "scalar":
                 nc.scalar.copy(out=dst, in_=src)
             else:
                 nc.vector.tensor_copy(out=dst, in_=src)
 
-        def whole_expert(e):
-            raw = landing_tile([P, PASSES, PACK * N], "raw%d" % e)
-            nc.sync.dma_start(out=raw[:], in_=w[e].rearrange("(o p j) n -> p o (j n)", p=P, j=PACK))
-            codes, scales, stage = mx_tiles(N, "%d" % e)
-            view = raw[:].rearrange("p o (j n) -> p o j n", j=PACK)
-            round_rows(view[:, :2], stage[:, : 2 * PACK * N], "scalar")
-            round_rows(view[:, 2:], stage[:, 2 * PACK * N :], "gpsimd")
-            quantize(codes, scales, stage, 0, 2 * N)
-            quantize(codes, scales, stage, 2 * N, 3 * N)
-            return codes, scales
+        def quantize(codes, scales, stage):
+            nc.vector.quantize_mx(out=codes.bitcast(FP8X4), scales=scales, in_=stage)
 
-        def half_expert(e, h):
-            raws = [landing_tile([P, PACK, P], "raw%d_%d_%d" % (e, h, o))[:] for o in range(PASSES)]
-            for o in range(PASSES):
-                nc.sync.dma_start(out=raws[o], in_=pass_rows(e, o, h * P, P))
-            codes, scales, stage = mx_tiles(P, "%d_%d" % (e, h))
-            if e == E - 1:
-                third = "vector"
-            elif h == 1:
-                third = "scalar" if e in SCALAR_ALONE else "vector"
-            else:
-                third = "gpsimd"
-            for o, engine in enumerate(("scalar", "scalar", third)):
-                round_rows(raws[o].unsqueeze(1), stage[:, PACK * o * P : PACK * (o + 1) * P], engine)
-            if e == E - 1:
-                quantize(codes, scales, stage, 0, 2 * P)
-                quantize(codes, scales, stage, 2 * P, 3 * P)
-            else:
-                quantize(codes, scales, stage, 0, PASSES * P)
-            return codes, scales
+        gathered = {}
 
         def gather_tokens(g):
-            slot_words = slot_pool.tile(
-                [P, PASSES * GATHER], U32, name="slot_words%d" % g, offset=g % SLOT_GROUPS * SLOT_BYTES, align_bytes=64
-            )
-            slot_planes = ring.tile([P, GATHER], U8, name="slot_planes", bufs=SLOT_GROUPS, align_bytes=64)
+            slot_words = placed(slot_pool, PASSES * GATHER, U32, "slot_words%d" % g, g % SLOT_GROUPS * SLOT_BYTES)
+            slot_planes = ring.tile([P, GATHER], U8, name="slot_planes", align_bytes=64)
             entries = offs_sb[:, g * GATHER // 16 : (g + 1) * GATHER // 16]
             for o in range(PASSES):
                 window = words[o].bitcast(U32)
                 nc.vector.tensor_copy(out=slot_words[:, o * GATHER : (o + 1) * GATHER], in_=window.indirect(entries))
             nc.vector.tensor_copy(out=slot_planes[:], in_=planes[:].indirect(entries))
-            return slot_words, slot_planes
+            gathered.setdefault(g, (slot_words, slot_planes))
 
-        gathered = {}
-
-        def product(acc, codes, scales, width, i, e, o):
+        def products(acc, codes, scales, width, i, e):
             g, first = divmod(e * C, GATHER)
-            if g not in gathered:
-                gathered.setdefault(g, gather_tokens(g))
             slot_words, slot_planes = gathered[g]
-            cols = slice(o * width + i * P, o * width + (i + 1) * P)
-            nc.tensor.matmul_mx(
-                out=acc,
-                lhsT=codes[:, cols].bitcast(FP8X4),
-                lhsT_scale=scales[:, cols],
-                rhs=slot_words[:, o * GATHER + first : o * GATHER + first + C].bitcast(FP8X4),
-                rhs_scale=slot_planes[4 * o :, first : first + C],
-                start=(o == 0),
-                stop=(o == PASSES - 1),
-            )
+            for o in range(PASSES):
+                cols = slice(o * width + i * P, o * width + (i + 1) * P)
+                nc.tensor.matmul_mx(
+                    out=acc,
+                    lhsT=codes[:, cols].bitcast(FP8X4),
+                    lhsT_scale=scales[:, cols],
+                    rhs=slot_words[:, o * GATHER + first : o * GATHER + first + C].bitcast(FP8X4),
+                    rhs_scale=slot_planes[4 * o :, first : first + C],
+                    start=(o == 0),
+                    stop=(o == PASSES - 1),
+                )
 
         def add_bias(acc, h, e0, count):
             nc.vector.tensor_tensor(
@@ -216,54 +158,7 @@ def tile_moe_shr_lin_bias_kernel(
                 op=ADD,
             )
 
-        def small_loads(e):
-            if e == 2:
-                nc.sync.dma_start(out=bias[:, :, : E + 1], in_=b.rearrange("(h p) e -> p h e", p=P))
-            if e == 0:
-                for q in range(4):
-                    nc.sync.dma_start(
-                        out=planes[32 * q : 32 * q + 4 * PASSES, :T].bitcast(I32),
-                        in_=x_scales[:, 4 * q : 4 * q + 4, :].bitcast(I32),
-                    )
-            if e in (4, 5):
-                for r in (2 * e - 8, 2 * e - 7):
-                    nc.sync.dma_start(out=pos_sb[r][:], in_=(pos1, pos2, pos3, pos4)[r])
-
-        def whole_run(e0, count, first_bank):
-            accs = [bank(first_bank + h, [P, count * C]) for h in range(HALVES)]
-            for n in range(count):
-                codes, scales = whole_expert(e0 + n)
-                small_loads(e0 + n)
-                for h in range(HALVES):
-                    for o in range(PASSES):
-                        product(accs[h][:, n * C : (n + 1) * C], codes, scales, N, h, e0 + n, o)
-            for h in range(HALVES):
-                add_bias(accs[h], h, e0, count)
-
-        def half_run(e0, count, h, number, after=None):
-            acc = bank(number, [P, count * C])
-            for n in range(count):
-                codes, scales = half_expert(e0 + n, h)
-                for o in range(PASSES):
-                    product(acc[:, n * C : (n + 1) * C], codes, scales, P, 0, e0 + n, o)
-                if after is not None:
-                    after(e0 + n)
-            add_bias(acc, h, e0, count)
-
-        def spread_gate():
-            turned = bank(4, [P, P])
-            nc.tensor.transpose(turned[:], gate_rows[:], ident[:])
-            nc.scalar.copy(out=gate_cols[:], in_=turned[:, : TOP * T // P])
-            flat = gate_sb[:].rearrange("p r t -> p (r t)")
-            for first in range(0, TOP * T // P, 4):
-                back = bank(5 + first // 4 % 3, [P, 4 * P])
-                for i in range(4):
-                    r, c = divmod(first + i, T // P)
-                    column = gate_cols[:, TOP * c + r : TOP * c + r + 1].to_broadcast([P, P])
-                    nc.tensor.transpose(back[:, i * P : (i + 1) * P], column, ident[:])
-                nc.scalar.copy(out=flat[:, first * P : (first + 4) * P], in_=back[:])
-
-        def turn(sources, numbers, spans, dst):
+        def turn(sources, numbers, spans):
             accs = [bank(number, [P, count]) for number, (t0, count) in zip(numbers, spans)]
             for r, source in enumerate(sources):
                 for acc, (t0, count) in zip(accs, spans):
@@ -272,10 +167,11 @@ def tile_moe_shr_lin_bias_kernel(
                             acc[:, c : c + P], lhsT=source[:, t0 + c : t0 + c + P], rhs=ident[:], is_transpose=True,
                             start=(r == 0 and c == 0), stop=(r == len(sources) - 1 and c == count - P),
                         )
-            if dst is not None:
-                for acc, (t0, count) in zip(accs, spans):
-                    nc.scalar.copy(out=dst[:, t0 : t0 + count], in_=acc[:])
             return accs
+
+        def copy_out(accs, spans, dst):
+            for acc, (t0, count) in zip(accs, spans):
+                nc.scalar.copy(out=dst[:, t0 : t0 + count], in_=acc[:])
 
         def fetched(h, r, t0, count):
             return y[h][:].indirect(pos_sb[r][:, t0 // 16 : (t0 + count) // 16])
@@ -285,46 +181,149 @@ def tile_moe_shr_lin_bias_kernel(
 
         nc.sync.dma_start(out=offs_sb[:], in_=offs)
         nc.sync.dma_start(out=all_words[:, :, :T], in_=x_words.rearrange("o p t r -> p o (t r)").bitcast(I32))
-        rows = gate[:, 0, :].rearrange("r (c t) -> c r t", t=P)
-        nc.scalar.dma_start(out=gate_rows[: TOP * T // P, :], in_=rows)
-        spread_gate()
+        nc.scalar.dma_start(out=gate_rows[: TOP * T // P, :], in_=gate[:, 0, :].rearrange("r (c t) -> c r t", t=P))
+        turned = bank(4, [P, P])
+        nc.tensor.transpose(turned[:], gate_rows[:], ident[:])
+        nc.scalar.copy(out=gate_cols[:], in_=turned[:, : TOP * T // P])
+        flat_gate = gate_sb[:].rearrange("p r t -> p (r t)")
+        for first in range(0, TOP * T // P, 4):
+            back = bank(5 + first // 4 % 3, [P, 4 * P])
+            for i in range(4):
+                r, c = divmod(first + i, T // P)
+                column = gate_cols[:, TOP * c + r : TOP * c + r + 1].to_broadcast([P, P])
+                nc.tensor.transpose(back[:, i * P : (i + 1) * P], column, ident[:])
+            nc.scalar.copy(out=flat_gate[:, first * P : (first + 4) * P], in_=back[:])
 
-        def behind(host, count, name):
-            return landing.tile([P, count], F32, name=name, offset=places[host], align_bytes=BUS)
+        def small_loads(e):
+            if e == 0:
+                for q in range(4):
+                    nc.sync.dma_start(
+                        out=planes[32 * q : 32 * q + 4 * PASSES, :T].bitcast(I32),
+                        in_=x_scales[:, 4 * q : 4 * q + 4, :].bitcast(I32),
+                    )
+            if e == 2:
+                nc.sync.dma_start(out=bias[:, :, : E + 1], in_=b.rearrange("(h p) e -> p h e", p=P))
+            if e in (4, 5):
+                for r in (2 * e - 8, 2 * e - 7):
+                    nc.sync.dma_start(out=pos_sb[r][:], in_=(pos1, pos2, pos3, pos4)[r])
 
-        for i, e0 in enumerate(range(0, WHOLE, RUN)):
-            whole_run(e0, min(RUN, WHOLE - e0), 2 * (i % 2))
-        for e0 in range(WHOLE, E, RUN):
-            half_run(e0, RUN, 0, e0 // RUN % 2)
-        terms = [keep.tile([P, T], F32, name="term0")]
-        fetch_weighed(0, 0, terms[0][:], 0, T)
+        for run, (e0, count) in enumerate(WHOLE_RUNS):
+            accs = [bank(run % 2 * HALVES + h, [P, count * C]) for h in range(HALVES)]
+            for e in range(e0, e0 + count):
+                raw = landing_tile([P, PASSES, PACK * N], "raw%d" % e)
+                nc.sync.dma_start(out=raw[:], in_=w[e].rearrange("(o p j) n -> p o (j n)", p=P, j=PACK))
+                small_loads(e)
+                slot = (e + LAST_SLOT - WHOLE + 1) % DEPTH
+                if e == 0:
+                    codes = placed(slot_pool, PASSES * N, U32, "codes0", 2 * SLOT_BYTES)
+                else:
+                    codes = placed(code_pool, PASSES * N, U32, "codes%d" % e, slot * 3 * KIB)
+                scales = placed(scale_pool, PASSES * N, U8, "scales%d" % e, slot * PASSES * N)
+                stage = placed(stages, PASSES * PACK * N, BF16, "stage%d" % e, slot * 6 * KIB)
+                view = raw[:].rearrange("p o (j n) -> p o j n", j=PACK)
+                round_rows(view[:, :2], stage[:, : 2 * PACK * N], "scalar")
+                cut = PACK * (2 * N + SCALAR_COLUMNS)
+                round_rows(view[:, 2:, :, :SCALAR_COLUMNS], stage[:, 2 * PACK * N : cut], "scalar")
+                round_rows(view[:, 2:, :, SCALAR_COLUMNS:], stage[:, cut:], "gpsimd")
+                quantize(codes[:, : 2 * N], scales[:, : 2 * N], stage[:, : 2 * PACK * N])
+                quantize(codes[:, 2 * N :], scales[:, 2 * N :], stage[:, 2 * PACK * N :])
+                if e % RUN == 0:
+                    gather_tokens(e // RUN)
+                for h in range(HALVES):
+                    products(accs[h][:, (e - e0) * C : (e - e0 + 1) * C], codes, scales, N, h, e)
+            for h in range(HALVES):
+                add_bias(accs[h], h, e0, count)
 
-        def next_term(e):
-            if e in TERM_HOSTS:
-                terms.append(behind("raw%d_1_1" % e, T, "term%d" % e))
-                fetch_weighed(0, len(terms) - 1, terms[-1][:], 0, T)
+        def half_expert(e, h):
+            name = "%d_%d" % (e, h)
+            i = e - WHOLE
+            if e == E - 1:
+                raws = [landing_tile([P, 1, PACK * P], "raw%s_%d" % (name, o))[:] for o in range(PASSES)]
+            else:
+                raw = landing_tile([P, PASSES, PACK * P], "raw" + name)
+                raws = [raw[:, o : o + 1] for o in range(PASSES)]
+                view = raw[:].rearrange("p o (j n) -> p o j n", j=PACK)
+            raws = [one.rearrange("p o (j n) -> p o j n", j=PACK) for one in raws]
+            for o in range(PASSES):
+                rows = w[e, o * P * PACK : (o + 1) * P * PACK, h * P : (h + 1) * P]
+                nc.sync.dma_start(out=raws[o][:, 0], in_=rows.rearrange("(p j) n -> p j n", j=PACK))
+            turn_of = i + h * (E - WHOLE)
+            codes = placed(code_pool, HALF_WORDS, U32, "codes" + name, HALF_CODES[(turn_of + 2 * h) % 4])
+            scales = placed(scale_pool, HALF_WORDS, U8, "scales" + name, HALF_SCALES[(turn_of + 3 * h) % 4])
+            if h == 0:
+                slot = i % 4
+            else:
+                slot = 4 + i % 6
+            places.setdefault(name, (slot * 3 * KIB, HALF_CODES[(turn_of + 2 * h) % 4]))
+            if e not in SCALAR_ALONE[h]:
+                first = placed(stages, 2 * PACK * P, BF16, "stage" + name, slot * 3 * KIB)
+                at = VECTOR_STAGE
+                if h == 1 and e % 2 == 1 and e < E - 1:
+                    at = VECTOR_STAGE - KIB
+                last = placed(stages, PACK * P, BF16, "last" + name, at + LAST_AT)
+                for o in range(2):
+                    round_rows(raws[o], first[:, o * PACK * P : (o + 1) * PACK * P], "scalar")
+                round_rows(raws[2], last[:], "vector")
+                quantize(codes[:, : 2 * P], scales[:, : 2 * P], first[:])
+                quantize(codes[:, 2 * P :], scales[:, 2 * P :], last[:])
+                return codes, scales
+            stage = placed(stages, PACK * HALF_WORDS, BF16, "stage" + name, slot * 3 * KIB)
+            if e == WHOLE:
+                for o in range(PASSES):
+                    round_rows(raws[o], stage[:, o * PACK * P : (o + 1) * PACK * P], "scalar")
+            else:
+                round_rows(view[:, :2], stage[:, : 2 * PACK * P], "scalar")
+                round_rows(view[:, 2:], stage[:, 2 * PACK * P :], "scalar")
+            quantize(codes[:], scales[:], stage[:])
+            return codes, scales
 
-        for e0 in range(WHOLE, E, RUN):
-            half_run(e0, RUN, 1, 2 + e0 // RUN % 2, next_term)
-        total = behind("raw19_1_0", T, "total")
-        turn(terms, (4, 5), TOKEN_PIECES, total)
+        def half_window(h, banks, after):
+            for number, (e0, count) in zip(banks, HALF_RUNS):
+                acc = bank(number, [P, count * C])
+                for e in range(e0, e0 + count):
+                    codes, scales = half_expert(e, h)
+                    if e // RUN not in gathered:
+                        gather_tokens(e // RUN)
+                    products(acc[:, (e - e0) * C : (e - e0 + 1) * C], codes, scales, P, 0, e)
+                    after(e)
+                add_bias(acc, h, e0, count)
+
+        places = {}
+        half_window(0, FIRST_BANKS, lambda e: None)
+
+        terms = [keep.tile([P, T], F32, name="term%d" % r) for r in range(TOP - 1)]
+        terms = terms + [placed(stages, T, F32, "term3", VECTOR_STAGE)]
+        for r in range(TOP):
+            fetch_weighed(0, r, terms[r][:], 0, T)
+        turned_sums = turn(terms, (4, 5), TOKEN_PIECES)
+
+        half_window(1, SECOND_BANKS, lambda e: None)
+        total = on_landing("raw%d_1_0" % (E - 1), T, "total")
+        copy_out(turned_sums, TOKEN_PIECES, total)
+        routed_banks = turn([total], (6, 7), TOKEN_PIECES)
 
         raws = []
         for o in range(PASSES):
             raw = landing_tile([P, PACK, N], "shared%d" % o)
-            nc.sync.dma_start(out=raw[:], in_=pass_rows(SHARED, o, 0, N))
+            rows = w[SHARED, o * P * PACK : (o + 1) * P * PACK, :]
+            nc.sync.dma_start(out=raw[:], in_=rows.rearrange("(p j) n -> p j n", j=PACK))
             raws.append(raw)
-        codes, scales, stage = mx_tiles(N, "shared")
+        codes = placed(code_pool, PASSES * N, U32, "codes_shared", min(places["18_1"][1], places["19_1"][1]))
+        scales = placed(scale_pool, PASSES * N, U8, "scales_shared", 0)
+        last_at = VECTOR_STAGE + LAST_AT
+        stage = [placed(stages, PACK * N, BF16, "stage_shared0", places["19_1"][0])]
+        stage = stage + [
+            placed(stages, PACK * N, BF16, "stage_shared%d" % o, last_at + KIB // 2 + 2 * KIB * (o - 2)) for o in (1, 2)
+        ]
         pieces = ((0, 0, 4 * P), (0, 4 * P, P), (1, 0, 2 * P), (1, 2 * P, P), (1, THROUGH, T - THROUGH))
         long_sums = bank(0, [P, 4 * P])
-        mixed_sums = bank(1, [P, 4 * P])
-        last_sums = bank(6, [P, T - THROUGH])
+        mixed_sums = bank(3, [P, 4 * P])
+        last_sums = bank(2, [P, T - THROUGH])
         homes = (long_sums[:], mixed_sums[:, :P], mixed_sums[:, P : 3 * P], mixed_sums[:, 3 * P :], last_sums[:])
-
-        def shared_pass(o):
+        for o in range(PASSES):
             round_rows(raws[o][:].unsqueeze(1), stage[o][:], "scalar")
             span = slice(o * N, (o + 1) * N)
-            nc.vector.quantize_mx(out=codes[:, span].bitcast(FP8X4), scales=scales[:, span], in_=stage[o][:])
+            quantize(codes[:, span], scales[:, span], stage[o][:])
             for i, (h, t0, count) in enumerate(pieces):
                 cols = slice(o * N + h * P, o * N + (h + 1) * P)
                 nc.tensor.matmul_mx(
@@ -346,16 +345,14 @@ def tile_moe_shr_lin_bias_kernel(
         plain = keep.tile([P, THROUGH], F32, name="plain")
         plain_rest = keep.tile([P, 2, rest], F32, name="plain_rest")
         results = [keep.tile([P, T], F32, name="result%d" % h, align_bytes=BUS) for h in range(HALVES)]
-        for o in range(PASSES):
-            shared_pass(o)
-        late_terms = [keep.tile([P, T], F32, name="late0"), behind("shared0", T, "late1")]
-        late_terms = late_terms + [behind("shared2", THROUGH, "late2"), keep.tile([P, THROUGH], F32, name="late3")]
+        late_terms = [keep.tile([P, T], F32, name="late0"), on_landing("shared0", T, "late1")]
+        late_terms = late_terms + [on_landing("shared2", THROUGH, "late2"), keep.tile([P, THROUGH], F32, name="late3")]
         rest_terms = keep.tile([P, 2, rest], F32, name="rest_terms")
         nc.scalar.activation(out=plain[:], in_=fetched(1, 3, 0, THROUGH), func=COPY)
         for r in (2, 3):
             nc.scalar.activation(out=plain_rest[:, r - 2, :], in_=fetched(1, r, THROUGH, rest), func=COPY)
-        routed0 = behind("shared1", T, "routed0")
-        turn([total], (3, 7), TOKEN_PIECES, routed0)
+        routed0 = on_landing("shared1", T, "routed0")
+        copy_out(routed_banks, TOKEN_PIECES, routed0)
         for r in (0, 1):
             fetch_weighed(1, r, late_terms[r][:], 0, T)
         fetch_weighed(1, 2, late_terms[2][:], 0, THROUGH)
@@ -364,8 +361,8 @@ def tile_moe_shr_lin_bias_kernel(
         routed1 = keep.tile([P, rest], F32, name="routed1")
         shared1 = keep.tile([P, THROUGH], F32, name="shared1")
         nc.scalar.activation(out=shared1[:], in_=mixed_sums[:, P:], func=IDENTITY, bias=bias[:, 1, SHARED : SHARED + 1])
-        turn(late_terms, (5,), ((0, THROUGH),), late_total)
-        (turned_back,) = turn([late_total], (4,), ((0, THROUGH),), None)
+        copy_out(turn(late_terms, (4,), ((0, THROUGH),)), ((0, THROUGH),), late_total)
+        (turned_back,) = turn([late_total], (5,), ((0, THROUGH),))
         steps = keep.tile([P, 2, rest], F32, name="steps")
         nc.vector.tensor_tensor(
             out=steps[:, 0, :], in0=late_terms[0][:, THROUGH:], in1=late_terms[1][:, THROUGH:], op=ADD

@@ -46,7 +46,7 @@ HALF_WORDS = PASSES * P
 LANDING_BYTES = 84 * KIB
 SLOT_GROUPS = 3
 SLOT_BYTES = 4 * PASSES * GATHER
-THROUGH = 3 * P
+THROUGH = 2 * P
 TOKEN_PIECES = ((0, 4 * P), (4 * P, P))
 HALF_CODES = (0, 3 * KIB // 2, 9 * KIB, 21 * KIB // 2)
 HALF_SCALES = (1536, 1920, 768, 1152)
@@ -315,11 +315,11 @@ def tile_moe_shr_lin_bias_kernel(
         stage = stage + [
             placed(stages, PACK * N, BF16, "stage_shared%d" % o, last_at + KIB // 2 + 2 * KIB * (o - 2)) for o in (1, 2)
         ]
-        pieces = ((0, 0, 4 * P), (0, 4 * P, P), (1, 0, 2 * P), (1, 2 * P, P), (1, THROUGH, T - THROUGH))
+        pieces = ((0, 0, 4 * P), (0, 4 * P, P), (1, 0, THROUGH), (1, THROUGH, 2 * P), (1, 4 * P, P))
         long_sums = bank(0, [P, 4 * P])
-        mixed_sums = bank(3, [P, 4 * P])
+        mixed_sums = bank(3, [P, P + THROUGH])
         last_sums = bank(2, [P, T - THROUGH])
-        homes = (long_sums[:], mixed_sums[:, :P], mixed_sums[:, P : 3 * P], mixed_sums[:, 3 * P :], last_sums[:])
+        homes = (long_sums[:], mixed_sums[:, :P], mixed_sums[:, P:], last_sums[:, : 2 * P], last_sums[:, 2 * P :])
         for o in range(PASSES):
             round_rows(raws[o][:].unsqueeze(1), stage[o][:], "scalar")
             span = slice(o * N, (o + 1) * N)
@@ -332,8 +332,8 @@ def tile_moe_shr_lin_bias_kernel(
                     lhsT_scale=scales[:, cols],
                     rhs=words[o][:, t0 : t0 + count].bitcast(FP8X4),
                     rhs_scale=planes[4 * o :, t0 : t0 + count],
-                    start=(o == 0 and i in (0, 1, 4)),
-                    stop=(o == PASSES - 1 and i in (0, 3, 4)),
+                    start=(o == 0 and i in (0, 1, 3)),
+                    stop=(o == PASSES - 1 and i in (0, 2, 4)),
                 )
 
         def add_shared(h, sums, routed, dst):
@@ -364,13 +364,13 @@ def tile_moe_shr_lin_bias_kernel(
         copy_out(turn(late_terms, (4,), ((0, THROUGH),)), ((0, THROUGH),), late_total)
         (turned_back,) = turn([late_total], (5,), ((0, THROUGH),))
         steps = keep.tile([P, 2, rest], F32, name="steps")
+        nc.vector.tensor_tensor(out=rest_terms[:], in0=plain_rest[:], in1=gate_sb[:, 2:, THROUGH:], op=MULT)
         nc.vector.tensor_tensor(
             out=steps[:, 0, :], in0=late_terms[0][:, THROUGH:], in1=late_terms[1][:, THROUGH:], op=ADD
         )
-        nc.vector.tensor_tensor(out=rest_terms[:], in0=plain_rest[:], in1=gate_sb[:, 2:, THROUGH:], op=MULT)
-        nc.vector.tensor_tensor(out=steps[:, 1, :], in0=steps[:, 0, :], in1=rest_terms[:, 0, :], op=ADD)
+        nc.vector.tensor_tensor(out=steps[:, 1, :], in0=rest_terms[:, 0, :], in1=rest_terms[:, 1, :], op=ADD)
         add_shared(0, homes[0], routed0[:, : 4 * P], results[0][:, : 4 * P])
-        nc.vector.tensor_tensor(out=routed1[:], in0=steps[:, 1, :], in1=rest_terms[:, 1, :], op=ADD)
+        nc.vector.tensor_tensor(out=routed1[:], in0=steps[:, 0, :], in1=steps[:, 1, :], op=ADD)
         add_shared(0, homes[1], routed0[:, 4 * P :], results[0][:, 4 * P :])
         nc.sync.dma_start(out=out[:P, :], in_=results[0][:])
         add_shared(1, last_sums[:], routed1[:], results[1][:, THROUGH:])

@@ -269,8 +269,8 @@ def tile_moe_shr_lin_bias_kernel(
                 return codes, scales
             stage = placed(stages, PACK * HALF_WORDS, BF16, "stage" + name, slot * 3 * KIB)
             if e == WHOLE:
-                for o in range(PASSES):
-                    round_rows(raws[o], stage[:, o * PACK * P : (o + 1) * PACK * P], "scalar")
+                for o, engine in enumerate(("scalar", "gpsimd" if h == 1 else "scalar", "scalar")):
+                    round_rows(raws[o], stage[:, o * PACK * P : (o + 1) * PACK * P], engine)
             else:
                 round_rows(view[:, :2], stage[:, : 2 * PACK * P], "scalar")
                 round_rows(view[:, 2:], stage[:, 2 * PACK * P :], "scalar")

from contextlib import ExitStack

import concourse.mybir as mybir
from concourse.masks import make_identity

K, T, E, C, N = 1536, 640, 20, 128, 256
TOP = 4
FLOPS = 2 * K * N * (E * C + T)

F32 = mybir.dt.float32
BF16 = mybir.dt.bfloat16
I32 = mybir.dt.int32
U32 = mybir.dt.uint32
U16 = mybir.dt.uint16
U8 = mybir.dt.uint8
FP8X4 = mybir.dt.float8_e4m3fn_x4
COPY = mybir.ActivationFunctionType.Copy
IDENTITY = mybir.ActivationFunctionType.Identity
MULT = mybir.AluOpType.mult
ADD = mybir.AluOpType.add

P = 128
PACK = 4
PASSES = K // (P * PACK)
HALVES = N // P
SLOTS = E * C
SHARED = E
GATHER = 512
RUN = 4
WINDOW = 704
BUS = 256
KIB = 1024
BANK_BYTES = 2 * KIB
WHOLE = 10
WHOLE_RUNS = ((0, 4), (4, 4), (8, 2))
HALF_RUNS = ((10, 4), (14, 4), (18, 2))
FIRST_BANKS = (2, 3, 0)
SECOND_BANKS = (2, 3, 1)
DEPTH = 5
LAST_SLOT = 2
SCALAR_ALONE = ((10, 12, 14, 16), (10, 11, 12, 13, 14, 15))
VECTOR_STAGE = 30 * KIB
SCALAR_COLUMNS = 96
LAST_AT = 3 * KIB // 2
HALF_WORDS = PASSES * P
LANDING_BYTES = 84 * KIB
SLOT_GROUPS = 3
SLOT_BYTES = 4 * PASSES * GATHER
THROUGH = 2 * P
TOKEN_PIECES = ((0, 4 * P), (4 * P, P))
HALF_CODES = (0, 3 * KIB // 2, 9 * KIB, 21 * KIB // 2)
HALF_SCALES = (1536, 1920, 768, 1152)


def tile_moe_shr_lin_bias_kernel(
    tc, x_words, x_scales, w, b, gate, offs, pos1, pos2, pos3, pos4, out
):
    nc = tc.nc
    with ExitStack() as ctx:
        keep = ctx.enter_context(tc.tile_pool(name="keep", bufs=1))
        ring = ctx.enter_context(tc.tile_pool(name="ring", bufs=SLOT_GROUPS))
        landing = ctx.enter_context(tc.tile_pool(name="landing", bufs=1))
        stages = ctx.enter_context(tc.tile_pool(name="stages", bufs=1))
        code_pool = ctx.enter_context(tc.tile_pool(name="code_pool", bufs=1))
        scale_pool = ctx.enter_context(tc.tile_pool(name="scale_pool", bufs=1))
        slot_pool = ctx.enter_context(tc.tile_pool(name="slot_pool", bufs=1))
        psum = ctx.enter_context(tc.psum_pool(name="psum", bufs=1))

        offs_sb = keep.tile([P, SLOTS // 16], U16, name="offs_sb")
        pos_sb = [keep.tile([P, T // 16], U16, name="pos_sb%d" % r) for r in range(TOP)]
        all_words = keep.tile([P, PASSES, WINDOW], I32, name="all_words", align_bytes=BUS)
        words = [all_words[:, o, :] for o in range(PASSES)]
        planes = keep.tile([P, WINDOW], U8, name="planes", align_bytes=64)
        bias = keep.tile([P, HALVES, 24], F32, name="bias")
        gate_rows = keep.tile([P, P], F32, name="gate_rows")
        gate_cols = keep.tile([P, TOP * T // P], F32, name="gate_cols")
        gate_sb = keep.tile([P, TOP, T], F32, name="gate_sb")
        ident = keep.tile([P, P], F32, name="ident")
        y = [keep.tile([P, SLOTS], F32, name="y%d" % h) for h in range(HALVES)]

        nc.vector.memset(planes[:].bitcast(I32), 0)
        nc.vector.memset(gate_rows[:], 0.0)
        nc.vector.memset(all_words[:, :, T:], 0)
        make_identity(nc, ident[:])

        banks_taken = []

        def bank(number, shape):
            banks_taken.append(number)
            return psum.tile(shape, F32, name="bank%d" % len(banks_taken), offset=number * BANK_BYTES)

        landed_at = {}
        landing_ends = [0]

        def landing_tile(shape, name):
            need = 4 * shape[1] * shape[2]
            start = landing_ends[-1] if landing_ends[-1] + need <= LANDING_BYTES else 0
            landing_ends.append(start + need)
            landed_at.setdefault(name, start)
            return landing.tile(shape, F32, name=name, offset=start, align_bytes=BUS)

        def placed(pool, count, dtype, name, offset):
            return pool.tile([P, count], dtype, name=name, offset=offset, align_bytes=64)

        def on_landing(host, count, name):
            return landing.tile([P, count], F32, name=name, offset=landed_at[host], align_bytes=BUS)

        def round_rows(raw, stage, engine):
            if engine == "gpsimd":
                nc.gpsimd.tensor_scalar(
                    out=stage.rearrange("p (o n j) -> p o n j", o=raw.shape[1], j=PACK),
                    in0=raw.rearrange("p o j n -> p o n j"),
                    scalar1=1.0, scalar2=0.0, op0=MULT, op1=ADD,
                )
                return
            dst = stage.rearrange("p (o c i j) -> p o c j i", o=raw.shape[1], i=4, j=PACK)
            src = raw.rearrange("p o j (c i) -> p o c j i", i=4)
            if engine == "scalar":
                nc.scalar.copy(out=dst, in_=src)
            else:
                nc.vector.tensor_copy(out=dst, in_=src)

        def quantize(codes, scales, stage):
            nc.vector.quantize_mx(out=codes.bitcast(FP8X4), scales=scales, in_=stage)

        gathered = {}

        def gather_tokens(g):
            slot_words = placed(slot_pool, PASSES * GATHER, U32, "slot_words%d" % g, g % SLOT_GROUPS * SLOT_BYTES)
            slot_planes = ring.tile([P, GATHER], U8, name="slot_planes", align_bytes=64)
            entries = offs_sb[:, g * GATHER // 16 : (g + 1) * GATHER // 16]
            for o in range(PASSES):
                window = words[o].bitcast(U32)
                nc.vector.tensor_copy(out=slot_words[:, o * GATHER : (o + 1) * GATHER], in_=window.indirect(entries))
            nc.vector.tensor_copy(out=slot_planes[:], in_=planes[:].indirect(entries))
            gathered.setdefault(g, (slot_words, slot_planes))

        def products(acc, codes, scales, width, i, e):
            g, first = divmod(e * C, GATHER)
            slot_words, slot_planes = gathered[g]
            for o in range(PASSES):
                cols = slice(o * width + i * P, o * width + (i + 1) * P)
                nc.tensor.matmul_mx(
                    out=acc,
                    lhsT=codes[:, cols].bitcast(FP8X4),
                    lhsT_scale=scales[:, cols],
                    rhs=slot_words[:, o * GATHER + first : o * GATHER + first + C].bitcast(FP8X4),
                    rhs_scale=slot_planes[4 * o :, first : first + C],
                    start=(o == 0),
                    stop=(o == PASSES - 1),
                )

        def add_bias(acc, h, e0, count):
            nc.vector.tensor_tensor(
                out=y[h][:, e0 * C : (e0 + count) * C].rearrange("p (e c) -> p e c", c=C),
                in0=acc[:].rearrange("p (e c) -> p e c", c=C),
                in1=bias[:, h, e0 : e0 + count].unsqueeze(2).to_broadcast([P, count, C]),
                op=ADD,
            )

        def turn(sources, numbers, spans):
            accs = [bank(number, [P, count]) for number, (t0, count) in zip(numbers, spans)]
            for r, source in enumerate(sources):
                for acc, (t0, count) in zip(accs, spans):
                    for c in range(0, count, P):
                        nc.tensor.matmul(
                            acc[:, c : c + P], lhsT=source[:, t0 + c : t0 + c + P], rhs=ident[:], is_transpose=True,
                            start=(r == 0 and c == 0), stop=(r == len(sources) - 1 and c == count - P),
                        )
            return accs

        def copy_out(accs, spans, dst):
            for acc, (t0, count) in zip(accs, spans):
                nc.scalar.copy(out=dst[:, t0 : t0 + count], in_=acc[:])

        def fetched(h, r, t0, count):
            return y[h][:].indirect(pos_sb[r][:, t0 // 16 : (t0 + count) // 16])

        def fetch_weighed(h, r, dst, t0, count):
            nc.vector.tensor_tensor(out=dst, in0=fetched(h, r, t0, count), in1=gate_sb[:, r, t0 : t0 + count], op=MULT)

        nc.sync.dma_start(out=offs_sb[:], in_=offs)
        nc.sync.dma_start(out=all_words[:, :, :T], in_=x_words.rearrange("o p t r -> p o (t r)").bitcast(I32))
        nc.scalar.dma_start(out=gate_rows[: TOP * T // P, :], in_=gate[:, 0, :].rearrange("r (c t) -> c r t", t=P))
        turned = bank(4, [P, P])
        nc.tensor.transpose(turned[:], gate_rows[:], ident[:])
        nc.scalar.copy(out=gate_cols[:], in_=turned[:, : TOP * T // P])
        flat_gate = gate_sb[:].rearrange("p r t -> p (r t)")
        for first in range(0, TOP * T // P, 4):
            back = bank(5 + first // 4 % 3, [P, 4 * P])
            for i in range(4):
                r, c = divmod(first + i, T // P)
                column = gate_cols[:, TOP * c + r : TOP * c + r + 1].to_broadcast([P, P])
                nc.tensor.transpose(back[:, i * P : (i + 1) * P], column, ident[:])
            nc.scalar.copy(out=flat_gate[:, first * P : (first + 4) * P], in_=back[:])

        def small_loads(e):
            if e == 0:
                for q in range(4):
                    nc.sync.dma_start(
                        out=planes[32 * q : 32 * q + 4 * PASSES, :T].bitcast(I32),
                        in_=x_scales[:, 4 * q : 4 * q + 4, :].bitcast(I32),
                    )
            if e == 2:
                nc.sync.dma_start(out=bias[:, :, : E + 1], in_=b.rearrange("(h p) e -> p h e", p=P))
            if e in (4, 5):
                for r in (2 * e - 8, 2 * e - 7):
                    nc.sync.dma_start(out=pos_sb[r][:], in_=(pos1, pos2, pos3, pos4)[r])

        for run, (e0, count) in enumerate(WHOLE_RUNS):
            accs = [bank(run % 2 * HALVES + h, [P, count * C]) for h in range(HALVES)]
            for e in range(e0, e0 + count):
                raw = landing_tile([P, PASSES, PACK * N], "raw%d" % e)
                nc.sync.dma_start(out=raw[:], in_=w[e].rearrange("(o p j) n -> p o (j n)", p=P, j=PACK))
                small_loads(e)
                slot = (e + LAST_SLOT - WHOLE + 1) % DEPTH
                if e == 0:
                    codes = placed(slot_pool, PASSES * N, U32, "codes0", 2 * SLOT_BYTES)
                else:
                    codes = placed(code_pool, PASSES * N, U32, "codes%d" % e, slot * 3 * KIB)
                scales = placed(scale_pool, PASSES * N, U8, "scales%d" % e, slot * PASSES * N)
                stage = placed(stages, PASSES * PACK * N, BF16, "stage%d" % e, slot * 6 * KIB)
                view = raw[:].rearrange("p o (j n) -> p o j n", j=PACK)
                round_rows(view[:, :2], stage[:, : 2 * PACK * N], "scalar")
                cut = PACK * (2 * N + SCALAR_COLUMNS)
                round_rows(view[:, 2:, :, :SCALAR_COLUMNS], stage[:, 2 * PACK * N : cut], "scalar")
                round_rows(view[:, 2:, :, SCALAR_COLUMNS:], stage[:, cut:], "gpsimd")
                quantize(codes[:, : 2 * N], scales[:, : 2 * N], stage[:, : 2 * PACK * N])
                quantize(codes[:, 2 * N :], scales[:, 2 * N :], stage[:, 2 * PACK * N :])
                if e % RUN == 0:
                    gather_tokens(e // RUN)
                for h in range(HALVES):
                    products(accs[h][:, (e - e0) * C : (e - e0 + 1) * C], codes, scales, N, h, e)
            for h in range(HALVES):
                add_bias(accs[h], h, e0, count)

        def half_expert(e, h):
            name = "%d_%d" % (e, h)
            i = e - WHOLE
            if e == E - 1:
                raws = [landing_tile([P, 1, PACK * P], "raw%s_%d" % (name, o))[:] for o in range(PASSES)]
            else:
                raw = landing_tile([P, PASSES, PACK * P], "raw" + name)
                raws = [raw[:, o : o + 1] for o in range(PASSES)]
                view = raw[:].rearrange("p o (j n) -> p o j n", j=PACK)
            raws = [one.rearrange("p o (j n) -> p o j n", j=PACK) for one in raws]
            for o in range(PASSES):
                rows = w[e, o * P * PACK : (o + 1) * P * PACK, h * P : (h + 1) * P]
                nc.sync.dma_start(out=raws[o][:, 0], in_=rows.rearrange("(p j) n -> p j n", j=PACK))
            turn_of = i + h * (E - WHOLE)
            codes = placed(code_pool, HALF_WORDS, U32, "codes" + name, HALF_CODES[(turn_of + 2 * h) % 4])
            scales = placed(scale_pool, HALF_WORDS, U8, "scales" + name, HALF_SCALES[(turn_of + 3 * h) % 4])
            if h == 0:
                slot = i % 4
            else:
                slot = 4 + i % 6
            places.setdefault(name, (slot * 3 * KIB, HALF_CODES[(turn_of + 2 * h) % 4]))
            if e not in SCALAR_ALONE[h]:
                first = placed(stages, 2 * PACK * P, BF16, "stage" + name, slot * 3 * KIB)
                at = VECTOR_STAGE
                if h == 1 and e % 2 == 1 and e < E - 1:
                    at = VECTOR_STAGE - KIB
                last = placed(stages, PACK * P, BF16, "last" + name, at + LAST_AT)
                for o in range(2):
                    round_rows(raws[o], first[:, o * PACK * P : (o + 1) * PACK * P], "scalar")
                round_rows(raws[2], last[:], "vector")
                quantize(codes[:, : 2 * P], scales[:, : 2 * P], first[:])
                quantize(codes[:, 2 * P :], scales[:, 2 * P :], last[:])
                return codes, scales
            stage = placed(stages, PACK * HALF_WORDS, BF16, "stage" + name, slot * 3 * KIB)
            if e == WHOLE:
                for o, engine in enumerate(("scalar", "gpsimd" if h == 1 else "scalar", "scalar")):
                    round_rows(raws[o], stage[:, o * PACK * P : (o + 1) * PACK * P], engine)
            else:
                round_rows(view[:, :2], stage[:, : 2 * PACK * P], "scalar")
                round_rows(view[:, 2:], stage[:, 2 * PACK * P :], "scalar")
            quantize(codes[:], scales[:], stage[:])
            return codes, scales

        def half_window(h, banks, after):
            for number, (e0, count) in zip(banks, HALF_RUNS):
                acc = bank(number, [P, count * C])
                for e in range(e0, e0 + count):
                    codes, scales = half_expert(e, h)
                    if e // RUN not in gathered:
                        gather_tokens(e // RUN)
                    products(acc[:, (e - e0) * C : (e - e0 + 1) * C], codes, scales, P, 0, e)
                    after(e)
                add_bias(acc, h, e0, count)

        places = {}
        half_window(0, FIRST_BANKS, lambda e: None)

        terms = [keep.tile([P, T], F32, name="term%d" % r) for r in range(TOP - 1)]
        terms = terms + [placed(stages, T, F32, "term3", VECTOR_STAGE)]
        for r in range(TOP):
            fetch_weighed(0, r, terms[r][:], 0, T)
        turned_sums = turn(terms, (4, 5), TOKEN_PIECES)

        half_window(1, SECOND_BANKS, lambda e: None)
        total = on_landing("raw%d_1_0" % (E - 1), T, "total")
        copy_out(turned_sums, TOKEN_PIECES, total)
        routed_banks = turn([total], (6, 7), TOKEN_PIECES)

        raws = []
        for o in range(PASSES):
            raw = landing_tile([P, PACK, N], "shared%d" % o)
            rows = w[SHARED, o * P * PACK : (o + 1) * P * PACK, :]
            nc.sync.dma_start(out=raw[:], in_=rows.rearrange("(p j) n -> p j n", j=PACK))
            raws.append(raw)
        codes = placed(code_pool, PASSES * N, U32, "codes_shared", min(places["18_1"][1], places["19_1"][1]))
        scales = placed(scale_pool, PASSES * N, U8, "scales_shared", 0)
        last_at = VECTOR_STAGE + LAST_AT
        stage = [placed(stages, PACK * N, BF16, "stage_shared0", places["19_1"][0])]
        stage = stage + [
            placed(stages, PACK * N, BF16, "stage_shared%d" % o, last_at + KIB // 2 + 2 * KIB * (o - 2)) for o in (1, 2)
        ]
        pieces = ((0, 0, 4 * P), (0, 4 * P, P), (1, 0, THROUGH), (1, THROUGH, 2 * P), (1, 4 * P, P))
        long_sums = bank(0, [P, 4 * P])
        mixed_sums = bank(3, [P, P + THROUGH])
        last_sums = bank(2, [P, T - THROUGH])
        homes = (long_sums[:], mixed_sums[:, :P], mixed_sums[:, P:], last_sums[:, : 2 * P], last_sums[:, 2 * P :])
        for o in range(PASSES):
            round_rows(raws[o][:].unsqueeze(1), stage[o][:], "scalar")
            span = slice(o * N, (o + 1) * N)
            quantize(codes[:, span], scales[:, span], stage[o][:])
            for i, (h, t0, count) in enumerate(pieces):
                cols = slice(o * N + h * P, o * N + (h + 1) * P)
                nc.tensor.matmul_mx(
                    out=homes[i],
                    lhsT=codes[:, cols].bitcast(FP8X4),
                    lhsT_scale=scales[:, cols],
                    rhs=words[o][:, t0 : t0 + count].bitcast(FP8X4),
                    rhs_scale=planes[4 * o :, t0 : t0 + count],
                    start=(o == 0 and i in (0, 1, 3)),
                    stop=(o == PASSES - 1 and i in (0, 2, 4)),
                )

        def add_shared(h, sums, routed, dst):
            nc.vector.scalar_tensor_tensor(
                out=dst, in0=sums, scalar=bias[:, h, SHARED : SHARED + 1], in1=routed, op0=ADD, op1=ADD
            )

        rest = T - THROUGH
        plain = keep.tile([P, THROUGH], F32, name="plain")
        plain_rest = keep.tile([P, 2, rest], F32, name="plain_rest")
        results = [keep.tile([P, T], F32, name="result%d" % h, align_bytes=BUS) for h in range(HALVES)]
        late_terms = [keep.tile([P, T], F32, name="late0"), on_landing("shared0", T, "late1")]
        late_terms = late_terms + [on_landing("shared2", THROUGH, "late2"), keep.tile([P, THROUGH], F32, name="late3")]
        rest_terms = keep.tile([P, 2, rest], F32, name="rest_terms")
        nc.scalar.activation(out=plain[:], in_=fetched(1, 3, 0, THROUGH), func=COPY)
        for r in (2, 3):
            nc.scalar.activation(out=plain_rest[:, r - 2, :], in_=fetched(1, r, THROUGH, rest), func=COPY)
        routed0 = on_landing("shared1", T, "routed0")
        copy_out(routed_banks, TOKEN_PIECES, routed0)
        for r in (0, 1):
            fetch_weighed(1, r, late_terms[r][:], 0, T)
        fetch_weighed(1, 2, late_terms[2][:], 0, THROUGH)
        nc.vector.tensor_tensor(out=late_terms[3][:], in0=plain[:], in1=gate_sb[:, 3, :THROUGH], op=MULT)
        late_total = keep.tile([P, THROUGH], F32, name="late_total")
        routed1 = keep.tile([P, rest], F32, name="routed1")
        shared1 = keep.tile([P, THROUGH], F32, name="shared1")
        nc.scalar.activation(out=shared1[:], in_=mixed_sums[:, P:], func=IDENTITY, bias=bias[:, 1, SHARED : SHARED + 1])
        copy_out(turn(late_terms, (4,), ((0, THROUGH),)), ((0, THROUGH),), late_total)
        (turned_back,) = turn([late_total], (5,), ((0, THROUGH),))
        steps = keep.tile([P, 2, rest], F32, name="steps")
        nc.vector.tensor_tensor(out=rest_terms[:], in0=plain_rest[:], in1=gate_sb[:, 2:, THROUGH:], op=MULT)
        nc.vector.tensor_tensor(
            out=steps[:, 0, :], in0=late_terms[0][:, THROUGH:], in1=late_terms[1][:, THROUGH:], op=ADD
        )
        nc.vector.tensor_tensor(out=steps[:, 1, :], in0=rest_terms[:, 0, :], in1=rest_terms[:, 1, :], op=ADD)
        add_shared(0, homes[0], routed0[:, : 4 * P], results[0][:, : 4 * P])
        nc.vector.tensor_tensor(out=routed1[:], in0=steps[:, 0, :], in1=steps[:, 1, :], op=ADD)
        add_shared(0, homes[1], routed0[:, 4 * P :], results[0][:, 4 * P :])
        nc.sync.dma_start(out=out[:P, :], in_=results[0][:])
        add_shared(1, last_sums[:], routed1[:], results[1][:, THROUGH:])
        nc.scalar.dma_start(out=out[P:, THROUGH:], in_=results[1][:, THROUGH:])
        nc.vector.tensor_tensor(out=results[1][:, :THROUGH], in0=turned_back[:], in1=shared1[:], op=ADD)
        nc.sync.dma_start(out=out[P:, :THROUGH], in_=results[1][:, :THROUGH])
